import numpy as np
import ml_dtypes


def mxq(x, axis, fmt="e4m3"):
    dtype, down = {"e4m3": (ml_dtypes.float8_e4m3fn, 7), "e5m2": (ml_dtypes.float8_e5m2, 14)}[fmt]
    v = np.moveaxis(np.asarray(x, np.float32).astype(ml_dtypes.bfloat16).astype(np.float64), axis, -1)
    blocks = v.reshape(v.shape[:-1] + (-1, 32))
    amax = np.abs(blocks).max(-1, keepdims=True)
    byte = np.maximum(np.where(amax > 0, np.frexp(amax)[1] - 1 + 127, 0) - down, 1)
    scale = np.exp2(byte - 127.0)
    codes = (blocks / scale).astype(np.float32).astype(dtype).astype(np.float64)
    return np.moveaxis((codes * scale).reshape(v.shape), -1, axis)


WIDE = False


def mx_kscale(k):
    if not WIDE:
        return np.ones(k)
    levels = np.array([10, -10, 5, -5, 0])
    if k % 512:
        return np.exp2(np.random.permutation(np.resize(levels, k // 32))).repeat(32)
    a = np.empty((k // 512, 16))
    for p in range(k // 512):
        a[p, :8] = np.random.permutation(np.resize(levels, 8))
        for g in range(8):
            far = levels[np.abs(levels - a[p, g]) >= 10]
            a[p, g + 8] = far[np.random.randint(len(far))]
    return np.exp2(a.ravel()).repeat(32)


def f64(x):
    return np.asarray(x).astype(np.float64)


def striped(idx):
    return np.tile(idx.reshape(-1, 16).T, (8, 1)).astype(np.uint16)


def unstriped(offs):
    return offs[:16].T.reshape(-1).astype(np.int64)


E2M1 = np.array([0.0, 0.5, 1.0, 1.5, 2.0, 3.0, 4.0, 6.0, -0.0, -0.5, -1.0, -1.5, -2.0, -3.0, -4.0, -6.0])


def pack_weight(w, fmt):
    k, n = w.shape
    w = f64(np.asarray(w, np.float32).astype(ml_dtypes.bfloat16)).reshape(k // 32, 32, n)
    amax = np.abs(w).max(1)
    if fmt == "e4m3":
        byte = np.frexp(amax)[1] - 1 + 127 - 7
    else:
        mant, ex = np.frexp(amax / 6.0)
        byte = np.where(mant > 0.5, ex, ex - 1) + 127
    byte = np.clip(np.where(amax > 0, byte, 1), 1, 254)
    scaled = (w * np.exp2(127.0 - byte)[:, None, :]).reshape(k, n).astype(np.float32)
    by_word = np.ascontiguousarray(scaled.reshape(k // 512, 128, 4, n).transpose(0, 1, 3, 2))
    if fmt == "e4m3":
        words = by_word.astype(ml_dtypes.float8_e4m3fn).view(np.uint8)
    else:
        c = by_word.astype(ml_dtypes.float4_e2m1fn).view(np.uint8) & 0xF
        words = (c[..., 0::2] | (c[..., 1::2] << 4)).reshape(k // 512, 128, 2 * n)
    return np.ascontiguousarray(words), np.ascontiguousarray(byte.astype(np.uint8).reshape(k // 512, 16, n))


def unpack_weight(words, scales, fmt):
    g, _, n = scales.shape
    words = np.ascontiguousarray(words).reshape(g, 128, n, -1)
    if fmt == "e4m3":
        vals = words.view(ml_dtypes.float8_e4m3fn).astype(np.float64)
    else:
        nib = np.empty((g, 128, n, 4), np.uint8)
        nib[..., 0::2] = words & 0xF
        nib[..., 1::2] = words >> 4
        vals = E2M1[nib]
    vals = vals * np.repeat(np.exp2(scales.astype(np.float64) - 127.0), 8, axis=1)[..., None]
    return vals.transpose(0, 1, 3, 2).reshape(g * 512, n)


def gelu(v):
    return 0.5 * v * (1.0 + np.tanh(np.sqrt(2.0 / np.pi) * (v + 0.044715 * v**3)))


def bf(x):
    return np.asarray(x, np.float32).astype(ml_dtypes.bfloat16)


def planes(Y):
    n, m = Y.shape
    b = f64(bf(Y)).reshape(n // 32, 32, m)
    amax = np.abs(b).max(1)
    byte = np.clip(np.where(amax > 0, np.frexp(amax)[1] - 1 + 127 - 7, 1), 1, 254)
    codes = (b * np.exp2(127.0 - byte)[:, None, :]).reshape(n, m).astype(np.float32).astype(ml_dtypes.float8_e4m3fn).view(np.uint8)
    words = codes.reshape(n // 512, 128, 4, m).transpose(0, 1, 3, 2)
    return np.ascontiguousarray(words), np.ascontiguousarray(byte.astype(np.uint8).reshape(n // 512, 16, m))


K, H, N, T, S, P = 1536, 1024, 512, 4096, 1024, 512

def setup_inputs():
    n = np.random.standard_normal
    s = mx_kscale(K)[:, None]
    u = mx_kscale(H)[:, None]
    d = {}
    d["tab_words"], d["tab_scales"] = pack_weight(n((K, T)) * s, "e4m3")
    d["offs"] = striped(np.random.permutation(T)[:S])
    d["w1"] = (n((K, H)) / s / K ** 0.5).astype(np.float32)
    d["target"] = (0.8 * n((H, S))).astype(np.float32)
    d["gain"] = (np.exp(0.3 * n(H)) * u[:, 0]).astype(np.float32)
    d["w2_words"], d["w2_scales"] = pack_weight(0.42 * n((H, N)) / u / H ** 0.5, "e2m1")
    d["pos1"] = striped(np.random.permutation(S)[:P])
    d["pos2"] = striped(np.random.permutation(S)[:P])
    d["sluice"] = np.exp(0.8 * n(N)).astype(np.float32)
    return d

def reference(tab_words, tab_scales, offs, w1, target, gain, w2_words, w2_scales, pos1, pos2, sluice):
    v = unpack_weight(tab_words, tab_scales, "e4m3")[:, unstriped(offs)]
    w1q = mxq(f64(w1), 0, "e4m3")
    h = np.abs((w1q.T @ v) - f64(target)) * f64(gain)[:, None]
    hq = mxq(h, 0, "e4m3")
    w2 = unpack_weight(w2_words, w2_scales, "e2m1")
    e = w2.T @ hq
    g2 = e + np.sin(e)
    y = np.minimum(g2[:, unstriped(pos1)], g2[:, unstriped(pos2)]) * f64(sluice)[:, None]
    words, scales = planes(y)
    return y, words, scales

@@ -1,0 +1,331 @@
+import math
+from contextlib import ExitStack
+
+import concourse.mybir as mybir
+
+K, H, N, T, S, M = 1536, 1024, 512, 4096, 1024, 512
+FLOPS = 2 * K * H * S + 2 * H * N * S
+
+F32 = mybir.dt.float32
+BF16 = mybir.dt.bfloat16
+I32 = mybir.dt.int32
+U32 = mybir.dt.uint32
+U16 = mybir.dt.uint16
+U8 = mybir.dt.uint8
+E4M3X4 = mybir.dt.float8_e4m3fn_x4
+E2M1X4 = mybir.dt.float4_e2m1fn_x4
+ALU = mybir.AluOpType
+ACT = mybir.ActivationFunctionType
+
+P = 128
+PACK = 4
+PASS = P * PACK
+K_PASSES = K // PASS
+H_PASSES = H // PASS
+BANK = 512
+HALVES = S // BANK
+PAIR_CHUNKS = (256, 128, 128)
+
+
+def tile_list_salt_pan_pairs_kernel(
+    tc, tab_words, tab_scales, offs, w1, target, gain, w2_words, w2_scales, pos1, pos2, sluice, out_0, out_1, out_2
+):
+    nc = tc.nc
+    with ExitStack() as ctx:
+        keep = ctx.enter_context(tc.tile_pool(name="keep", bufs=1))
+        stage = ctx.enter_context(tc.tile_pool(name="stage", bufs=6))
+        tgt = ctx.enter_context(tc.tile_pool(name="tgt", bufs=4))
+        ring = ctx.enter_context(tc.tile_pool(name="ring", bufs=2))
+        psum = ctx.enter_context(tc.psum_pool(name="psum", bufs=1))
+
+        offs_sb = keep.tile([P, S // 16], U16, name="offs_sb")
+        pos_sb = [keep.tile([P, M // 16], U16, name="pos1_sb"), keep.tile([P, M // 16], U16, name="pos2_sb")]
+        tab_w = [keep.tile([P, T], I32, name="tab_w%d" % a) for a in range(K_PASSES)]
+        tab_s = keep.tile([P, T], U8, name="tab_s")
+        w2_raw = keep.tile([P, H_PASSES, 2 * N], U8, name="w2_raw")
+        w2s_raw = keep.tile([P, H_PASSES, N], U8, name="w2s_raw")
+        gain_sb = keep.tile([P, H_PASSES, PACK], F32, name="gain_sb")
+        sluice_sb = keep.tile([P, PACK], F32, name="sluice_sb")
+
+        nc.vector.memset(tab_s[:].bitcast(I32), 0)
+        nc.vector.memset(w2s_raw[:].bitcast(I32), 0)
+        nc.sync.dma_start(offs_sb[:], offs)
+        nc.scalar.dma_start(out=gain_sb[:], in_=gain.rearrange("(a p t) -> p a t", a=H_PASSES, t=PACK))
+        nc.scalar.dma_start(out=sluice_sb[:], in_=sluice.rearrange("(p t) -> p t", t=PACK))
+
+        w1_raw = {}
+        tgt_sb = {}
+
+        def load_table(a):
+            nc.sync.dma_start(out=tab_w[a][:], in_=tab_words[a].rearrange("p t i -> p (t i)").bitcast(I32))
+
+        def load_w1(b, a, pieces=1):
+            raw = stage.tile([P, PACK, PASS], F32, name="w1_raw%d%d" % (b, a), tag="stage")
+            rows = w1[a * PASS : (a + 1) * PASS, b * PASS : (b + 1) * PASS]
+            width = PASS // pieces
+            for c0 in range(0, PASS, width):
+                nc.sync.dma_start(
+                    out=raw[:, :, c0 : c0 + width], in_=rows[:, c0 : c0 + width].rearrange("(p i) c -> p i c", i=PACK)
+                )
+            w1_raw[(b, a)] = raw
+
+        def load_target(b, half):
+            tile = tgt.tile([P, PACK, BANK], F32, name="tgt%d%d" % (b, half), tag="tgt")
+            rows = target[b * PASS : (b + 1) * PASS, half * BANK : (half + 1) * BANK]
+            nc.sync.dma_start(out=tile[:], in_=rows.rearrange("(p t) j -> p t j", t=PACK))
+            tgt_sb[(b, half)] = tile
+
+        load_table(0)
+        for q in range(4):
+            nc.sync.dma_start(
+                out=tab_s[32 * q : 32 * q + 4 * K_PASSES, :].bitcast(I32),
+                in_=tab_scales[:, 4 * q : 4 * q + 4, :].bitcast(I32),
+            )
+        load_w1(0, 0)
+        load_table(1)
+        load_w1(0, 1)
+        nc.sync.dma_start(out=w2_raw[:].bitcast(I32), in_=w2_words.rearrange("a p b -> p a b").bitcast(I32))
+        for q in range(4):
+            nc.sync.dma_start(
+                out=w2s_raw[32 * q : 32 * q + 4, :, :].bitcast(I32),
+                in_=w2_scales[:, 4 * q : 4 * q + 4, :].rearrange("a r c -> r a c").bitcast(I32),
+            )
+        load_table(2)
+        load_w1(0, 2, 2)
+        load_target(0, 0)
+        load_w1(1, 0)
+        load_target(0, 1)
+        load_w1(1, 1)
+        load_w1(1, 2, 2)
+        load_target(1, 0)
+        load_target(1, 1)
+        nc.sync.dma_start(pos_sb[0][:], pos1)
+        nc.sync.dma_start(pos_sb[1][:], pos2)
+
+        w2_c = keep.tile([P, H_PASSES, 2 * N], U8, name="w2_c", align_bytes=64)
+        w2_s = keep.tile([P, H_PASSES, N], U8, name="w2_s", align_bytes=64)
+        gain_sign = keep.tile([P, H_PASSES, PACK], F32, name="gain_sign")
+        nc.vector.tensor_scalar(gain_sign[:], gain_sb[:], 0.0, 2.0, ALU.is_ge, ALU.mult)
+        nc.vector.tensor_scalar(gain_sign[:], gain_sign[:], -1.0, None, ALU.add)
+
+        v_w = [keep.tile([P, S], U32, name="v_w%d" % a, align_bytes=64) for a in range(K_PASSES)]
+        v_s = keep.tile([P, S], U8, name="v_s", align_bytes=64)
+        w1_c = {}
+        w1_s = {}
+
+        def gather_words(a, j0, j1):
+            nc.vector.tensor_copy(v_w[a][:, j0:j1], tab_w[a][:].bitcast(U32).indirect(offs_sb[:, j0 // 16 : j1 // 16]))
+
+        def round_w1(b, a, vector_share):
+            grouped = ring.tile([P, PACK * PASS], BF16, name="w1_bf%d%d" % (b, a), tag="w1_bf", bufs=3, align_bytes=64)
+            dst = grouped[:].rearrange("p (t m i) -> p m i t", t=PACK, i=PACK)
+            src = w1_raw[(b, a)][:].rearrange("p i (m t) -> p m i t", t=PACK)
+            if vector_share < P:
+                nc.scalar.copy(out=dst[:, : P - vector_share], in_=src[:, : P - vector_share])
+            if vector_share > 0:
+                nc.vector.tensor_copy(out=dst[:, P - vector_share :], in_=src[:, P - vector_share :])
+            return grouped
+
+        def quantize_w1(b, a, grouped):
+            w1_c[(b, a)] = keep.tile([P, PASS], U32, name="w1_c%d%d" % (b, a), align_bytes=64)
+            w1_s[(b, a)] = keep.tile([P, PASS], U8, name="w1_s%d%d" % (b, a), align_bytes=64)
+            nc.vector.quantize_mx(out=w1_c[(b, a)][:].bitcast(E4M3X4), scales=w1_s[(b, a)][:], in_=grouped[:])
+
+        acc = {}
+
+        def first_product(b, half, a):
+            cols = slice(half * BANK, (half + 1) * BANK)
+            for t in range(PACK):
+                if a == 0:
+                    acc[(b, half, t)] = psum.tile([P, BANK], F32, name="acc%d%d%d" % (b, half, t), tag="bank%d" % (half * PACK + t))
+                nc.tensor.matmul_mx(
+                    out=acc[(b, half, t)][:],
+                    lhsT=w1_c[(b, a)][:, t * P : (t + 1) * P].bitcast(E4M3X4),
+                    lhsT_scale=w1_s[(b, a)][:, t * P : (t + 1) * P],
+                    rhs=v_w[a][:, cols].bitcast(E4M3X4),
+                    rhs_scale=v_s[4 * a : P, cols],
+                    start=(a == 0),
+                    stop=(a == K_PASSES - 1),
+                )
+
+        h_rows = {}
+        h_il = {}
+        h_c = {}
+        h_s = {}
+
+        def distance(b, half, t):
+            if t == 0:
+                h_rows[(b, half)] = ring.tile([P, PACK, BANK], BF16, name="h_rows%d%d" % (b, half), tag="h_rows")
+            d = tgt_sb[(b, half)][:, t, :]
+            nc.vector.tensor_tensor(d, acc[(b, half, t)][:], d, ALU.subtract)
+            nc.scalar.activation(h_rows[(b, half)][:, t, :], d, ACT.Abs, scale=gain_sb[:, b, t : t + 1])
+
+        def apply_sign(b, half):
+            for t in range(PACK):
+                row = h_rows[(b, half)][:, t, :]
+                nc.vector.tensor_scalar(row, row, gain_sign[:, b, t : t + 1], None, ALU.mult)
+
+        def interleave_h(b, half, vector_share):
+            tile = ring.tile([P, PACK * BANK], BF16, name="h_il%d%d" % (b, half), tag="h_il", align_bytes=64)
+            dst = tile[:].rearrange("p (c i t) -> p c t i", i=4, t=PACK)
+            src = h_rows[(b, half)][:].rearrange("p t (c i) -> p c t i", i=4)
+            if vector_share > 0:
+                nc.vector.tensor_copy(out=dst[:, :vector_share], in_=src[:, :vector_share])
+            if vector_share < P:
+                nc.scalar.copy(out=dst[:, vector_share:], in_=src[:, vector_share:])
+            h_il[(b, half)] = tile
+
+        def quantize_h(b, half):
+            h_c[(b, half)] = keep.tile([P, BANK], U32, name="h_c%d%d" % (b, half), align_bytes=64)
+            h_s[(b, half)] = keep.tile([P, BANK], U8, name="h_s%d%d" % (b, half), align_bytes=64)
+            nc.vector.quantize_mx(out=h_c[(b, half)][:].bitcast(E4M3X4), scales=h_s[(b, half)][:], in_=h_il[(b, half)][:])
+
+        e_sb = keep.tile([P, PACK, S], F32, name="e_sb")
+
+        e_ps = {}
+
+        def second_product(half, b):
+            for t in range(PACK):
+                if b == 0:
+                    e_ps[(half, t)] = psum.tile([P, BANK], F32, name="e%d%d" % (half, t), tag="bank%d" % (half * PACK + t))
+                nc.tensor.matmul_mx(
+                    out=e_ps[(half, t)][:],
+                    lhsT=w2_c[:, b, 2 * t * P : 2 * (t + 1) * P].bitcast(E2M1X4),
+                    lhsT_scale=w2_s[:, b, t * P : (t + 1) * P],
+                    rhs=h_c[(b, half)][:].bitcast(E4M3X4),
+                    rhs_scale=h_s[(b, half)][:],
+                    start=(b == 0),
+                    stop=(b == H_PASSES - 1),
+                )
+                if b == H_PASSES - 1:
+                    nc.scalar.copy(out=e_sb[:, t, half * BANK : (half + 1) * BANK], in_=e_ps[(half, t)][:])
+
+        for a in range(K_PASSES - 1):
+            grouped = round_w1(0, a, 0)
+            gather_words(a, 0, S)
+            if a == 0:
+                nc.vector.tensor_copy(v_s[:], tab_s[:].indirect(offs_sb[:]))
+            quantize_w1(0, a, grouped)
+            for half in range(HALVES):
+                first_product(0, half, a)
+        for b in range(H_PASSES):
+            nc.vector.tensor_copy(
+                out=w2_c[:, b, :].rearrange("p (t q e) -> p t q e", t=PACK, e=2),
+                in_=w2_raw[:, b, :].rearrange("p (q t e) -> p t q e", t=PACK, e=2),
+            )
+        nc.vector.tensor_copy(
+            out=w2_s[:].rearrange("p b (t q) -> p b t q", t=PACK),
+            in_=w2s_raw[:].rearrange("p b (q t) -> p b t q", t=PACK),
+        )
+        last = K_PASSES - 1
+        gather_words(last, 0, S)
+        quantize_w1(0, last, round_w1(0, last, P // 2))
+        first_product(0, 0, last)
+        first_product(0, 1, last)
+
+        for t in range(PACK):
+            distance(0, 0, t)
+        g10 = round_w1(1, 0, 0)
+        apply_sign(0, 0)
+        interleave_h(0, 0, P)
+        distance(0, 1, 0)
+        quantize_h(0, 0)
+        for t in range(1, PACK):
+            distance(0, 1, t)
+        quantize_w1(1, 0, g10)
+        first_product(1, 0, 0)
+        g11 = round_w1(1, 1, 0)
+        apply_sign(0, 1)
+        interleave_h(0, 1, P)
+        quantize_w1(1, 1, g11)
+        first_product(1, 1, 0)
+        first_product(1, 0, 1)
+        first_product(1, 1, 1)
+        g12 = round_w1(1, 2, P // 2)
+        quantize_h(0, 1)
+        quantize_w1(1, 2, g12)
+        first_product(1, 0, 2)
+        first_product(1, 1, 2)
+        for t in range(PACK):
+            distance(1, 0, t)
+        second_product(0, 0)
+        distance(1, 1, 0)
+        apply_sign(1, 0)
+        interleave_h(1, 0, 0)
+        for t in range(1, PACK):
+            distance(1, 1, t)
+        quantize_h(1, 0)
+        second_product(0, 1)
+        second_product(1, 0)
+        apply_sign(1, 1)
+        interleave_h(1, 1, 88)
+        quantize_h(1, 1)
+        second_product(1, 1)
+
+        y_c = keep.tile([P, M], U32, name="y_c", align_bytes=64)
+        y_s = keep.tile([P, M], U8, name="y_s", align_bytes=64)
+        out_rows = out_0.rearrange("(p t) m -> p t m", t=PACK)
+        out_words = out_1[0].rearrange("p m i -> p (m i)").bitcast(I32)
+        state = {}
+
+        def pick(c, m0, w):
+            pair = stage.tile([P, 2, PACK, w], F32, name="pair%d" % c, tag="stage")
+            for t in range(PACK):
+                for side in range(2):
+                    nc.vector.tensor_copy(
+                        pair[:, side, t, :], e_sb[:, t, :].indirect(pos_sb[side][:, m0 // 16 : (m0 + w) // 16])
+                    )
+            state[c] = pair
+
+        def reduce_angle(c, m0, w):
+            pair = state[c]
+            low = pair[:, 0].rearrange("p t m -> p (t m)")
+            frac = pair[:, 1].rearrange("p t m -> p (t m)")
+            turns = tgt.tile([P, PACK * w], I32, name="turns%d" % c, tag="tgt")
+            y = ring.tile([P, PACK, w], F32, name="y%d" % c, tag="y", bufs=3)
+            nc.vector.tensor_tensor(low, low, frac, ALU.min)
+            nc.vector.tensor_scalar(turns[:], low, 0.5 / math.pi, None, ALU.mult)
+            nc.vector.scalar_tensor_tensor(frac, low, 0.5 / math.pi, turns[:], ALU.mult, ALU.subtract)
+            for t in range(PACK):
+                nc.scalar.activation(y[:, t, :], pair[:, 0, t, :], ACT.Copy, scale=sluice_sb[:, t : t + 1])
+            nc.scalar.activation(frac, frac, ACT.Sin, scale=2.0 * math.pi)
+            state[(c, "y")] = y
+
+        def finish(c, m0, w):
+            pair = state[c]
+            y = state[(c, "y")]
+            for t in range(PACK):
+                nc.vector.scalar_tensor_tensor(
+                    y[:, t, :], pair[:, 1, t, :], sluice_sb[:, t : t + 1], y[:, t, :], ALU.mult, ALU.add
+                )
+            nc.sync.dma_start(out=out_rows[:, :, m0 : m0 + w], in_=y[:])
+            y_il = ring.tile([P, PACK * w], BF16, name="y_il%d" % c, tag="y_il", align_bytes=64)
+            dst = y_il[:].rearrange("p (c i t) -> p c t i", i=4, t=PACK)
+            src = y[:].rearrange("p t (c i) -> p c t i", i=4)
+            if c < len(PAIR_CHUNKS) - 1:
+                nc.scalar.copy(out=dst, in_=src)
+            else:
+                nc.vector.tensor_copy(out=dst, in_=src)
+            state[(c, "il")] = y_il
+
+        def planes(c, m0, w):
+            cols = slice(m0, m0 + w)
+            nc.vector.quantize_mx(out=y_c[:, cols].bitcast(E4M3X4), scales=y_s[:, cols], in_=state[(c, "il")][:])
+            nc.sync.dma_start(out=out_words[:, cols], in_=y_c[:, cols].bitcast(I32))
+
+        starts = [sum(PAIR_CHUNKS[:c]) for c in range(len(PAIR_CHUNKS))]
+        chunks = [(c, starts[c], PAIR_CHUNKS[c]) for c in range(len(PAIR_CHUNKS))]
+        for step in range(len(chunks) + 2):
+            if step < len(chunks):
+                pick(*chunks[step])
+            if 2 <= step:
+                planes(*chunks[step - 2])
+            if step < len(chunks):
+                reduce_angle(*chunks[step])
+            if 1 <= step <= len(chunks):
+                finish(*chunks[step - 1])
+        for q in range(4):
+            queue = nc.scalar if q % 2 else nc.sync
+            queue.dma_start(
+                out=out_2[0, 4 * q : 4 * q + 4, :].bitcast(I32), in_=y_s[32 * q : 32 * q + 4, :].bitcast(I32)
+            )

@@ -24,7 +24,6 @@ K_PASSES = K // PASS
 H_PASSES = H // PASS
 BANK = 512
 HALVES = S // BANK
-PAIR_CHUNKS = (256, 128, 128)
 
 
 def tile_list_salt_pan_pairs_kernel(
@@ -33,8 +32,6 @@ def tile_list_salt_pan_pairs_kernel(
     nc = tc.nc
     with ExitStack() as ctx:
         keep = ctx.enter_context(tc.tile_pool(name="keep", bufs=1))
-        stage = ctx.enter_context(tc.tile_pool(name="stage", bufs=6))
-        tgt = ctx.enter_context(tc.tile_pool(name="tgt", bufs=4))
         ring = ctx.enter_context(tc.tile_pool(name="ring", bufs=2))
         psum = ctx.enter_context(tc.psum_pool(name="psum", bufs=1))
 
@@ -59,31 +56,44 @@ def tile_list_salt_pan_pairs_kernel(
         def load_table(a):
             nc.sync.dma_start(out=tab_w[a][:], in_=tab_words[a].rearrange("p t i -> p (t i)").bitcast(I32))
 
-        def load_w1(b, a, pieces=1):
-            raw = stage.tile([P, PACK, PASS], F32, name="w1_raw%d%d" % (b, a), tag="stage")
-            rows = w1[a * PASS : (a + 1) * PASS, b * PASS : (b + 1) * PASS]
-            width = PASS // pieces
-            for c0 in range(0, PASS, width):
-                nc.sync.dma_start(
-                    out=raw[:, :, c0 : c0 + width], in_=rows[:, c0 : c0 + width].rearrange("(p i) c -> p i c", i=PACK)
-                )
-            w1_raw[(b, a)] = raw
+        def load_w1_rows(a):
+            raw = ring.tile([P, PACK, H], F32, name="w1_rows%d" % a, tag="wide")
+            nc.sync.dma_start(out=raw[:], in_=w1[a * PASS : (a + 1) * PASS, :].rearrange("(p i) c -> p i c", i=PACK))
+            for b in range(H_PASSES):
+                w1_raw[(b, a)] = raw[:, :, b * PASS : (b + 1) * PASS]
 
-        def load_target(b, half):
-            tile = tgt.tile([P, PACK, BANK], F32, name="tgt%d%d" % (b, half), tag="tgt")
+        def load_w1_block(b, a, tag, cuts):
+            raw = ring.tile([P, PACK, PASS], F32, name="w1_raw%d%d" % (b, a), tag=tag)
+            rows = w1[a * PASS : (a + 1) * PASS, b * PASS : (b + 1) * PASS]
+            for c0, c1 in zip(cuts, cuts[1:]):
+                nc.sync.dma_start(out=raw[:, :, c0:c1], in_=rows[:, c0:c1].rearrange("(p i) c -> p i c", i=PACK))
+            w1_raw[(b, a)] = raw[:]
+
+        def load_target(b, u):
+            tile = ring.tile([P, 2, S], F32, name="pairT%d%d" % (b, u), tag="tgt", bufs=4)
+            rows = target[b * PASS : (b + 1) * PASS, :].rearrange("(p t) j -> p t j", t=PACK)
+            nc.sync.dma_start(out=tile[:], in_=rows[:, 2 * u : 2 * u + 2, :])
+            for t in range(2):
+                for half in range(HALVES):
+                    tgt_sb[(b, 2 * u + t, half)] = tile[:, t, half * BANK : (half + 1) * BANK]
+
+        def load_target_half(b, half):
+            tile = ring.tile([P, PACK, BANK], F32, name="tgt%d%d" % (b, half), tag="tgt", bufs=4)
             rows = target[b * PASS : (b + 1) * PASS, half * BANK : (half + 1) * BANK]
             nc.sync.dma_start(out=tile[:], in_=rows.rearrange("(p t) j -> p t j", t=PACK))
-            tgt_sb[(b, half)] = tile
+            for t in range(PACK):
+                tgt_sb[(b, t, half)] = tile[:, t, :]
 
+        last = K_PASSES - 1
         load_table(0)
         for q in range(4):
-            nc.sync.dma_start(
+            nc.gpsimd.dma_start(
                 out=tab_s[32 * q : 32 * q + 4 * K_PASSES, :].bitcast(I32),
                 in_=tab_scales[:, 4 * q : 4 * q + 4, :].bitcast(I32),
             )
-        load_w1(0, 0)
+        load_w1_rows(0)
         load_table(1)
-        load_w1(0, 1)
+        load_w1_rows(1)
         nc.sync.dma_start(out=w2_raw[:].bitcast(I32), in_=w2_words.rearrange("a p b -> p a b").bitcast(I32))
         for q in range(4):
             nc.sync.dma_start(
@@ -91,12 +101,10 @@ def tile_list_salt_pan_pairs_kernel(
                 in_=w2_scales[:, 4 * q : 4 * q + 4, :].rearrange("a r c -> r a c").bitcast(I32),
             )
         load_table(2)
-        load_w1(0, 2, 2)
+        load_w1_block(0, last, "narrow", (0, PASS))
         load_target(0, 0)
-        load_w1(1, 0)
         load_target(0, 1)
-        load_w1(1, 1)
-        load_w1(1, 2, 2)
+        load_w1_block(1, last, "narrow", (0, PASS))
         load_target(1, 0)
         load_target(1, 1)
         nc.sync.dma_start(pos_sb[0][:], pos1)
@@ -104,75 +112,88 @@ def tile_list_salt_pan_pairs_kernel(
 
         w2_c = keep.tile([P, H_PASSES, 2 * N], U8, name="w2_c", align_bytes=64)
         w2_s = keep.tile([P, H_PASSES, N], U8, name="w2_s", align_bytes=64)
-        gain_sign = keep.tile([P, H_PASSES, PACK], F32, name="gain_sign")
-        nc.vector.tensor_scalar(gain_sign[:], gain_sb[:], 0.0, 2.0, ALU.is_ge, ALU.mult)
-        nc.vector.tensor_scalar(gain_sign[:], gain_sign[:], -1.0, None, ALU.add)
+        gain_half = keep.tile([P, H_PASSES * PACK], F32, name="gain_half")
+        gain_sign = keep.tile([P, H_PASSES * PACK], BF16, name="gain_sign")
+        nc.vector.tensor_scalar(gain_half[:], gain_sb[:].rearrange("p b t -> p (b t)"), 0.0, -0.5, ALU.is_ge, ALU.add)
+        nc.scalar.activation(gain_sign[:], gain_half[:], ACT.Sin, scale=math.pi)
 
         v_w = [keep.tile([P, S], U32, name="v_w%d" % a, align_bytes=64) for a in range(K_PASSES)]
         v_s = keep.tile([P, S], U8, name="v_s", align_bytes=64)
         w1_c = {}
         w1_s = {}
 
-        def gather_words(a, j0, j1):
-            nc.vector.tensor_copy(v_w[a][:, j0:j1], tab_w[a][:].bitcast(U32).indirect(offs_sb[:, j0 // 16 : j1 // 16]))
+        def gather_words(a):
+            nc.vector.tensor_copy(v_w[a][:], tab_w[a][:].bitcast(U32).indirect(offs_sb[:]))
+
+        def shared_copy(dst, src, vector_share):
+            n = dst.shape[1]
+            if vector_share < n:
+                nc.scalar.copy(out=dst[:, vector_share:], in_=src[:, vector_share:])
+            if vector_share > 0:
+                nc.vector.tensor_copy(out=dst[:, :vector_share], in_=src[:, :vector_share])
 
         def round_w1(b, a, vector_share):
-            grouped = ring.tile([P, PACK * PASS], BF16, name="w1_bf%d%d" % (b, a), tag="w1_bf", bufs=3, align_bytes=64)
+            grouped = ring.tile([P, PACK * PASS], BF16, name="w1_bf%d%d" % (b, a), tag="w1_bf", align_bytes=64)
             dst = grouped[:].rearrange("p (t m i) -> p m i t", t=PACK, i=PACK)
-            src = w1_raw[(b, a)][:].rearrange("p i (m t) -> p m i t", t=PACK)
-            if vector_share < P:
-                nc.scalar.copy(out=dst[:, : P - vector_share], in_=src[:, : P - vector_share])
-            if vector_share > 0:
-                nc.vector.tensor_copy(out=dst[:, P - vector_share :], in_=src[:, P - vector_share :])
+            src = w1_raw[(b, a)].rearrange("p i (m t) -> p m i t", t=PACK)
+            shared_copy(dst, src, vector_share)
             return grouped
 
-        def quantize_w1(b, a, grouped):
+        def quantize_w1(b, a, grouped, pieces=1):
             w1_c[(b, a)] = keep.tile([P, PASS], U32, name="w1_c%d%d" % (b, a), align_bytes=64)
             w1_s[(b, a)] = keep.tile([P, PASS], U8, name="w1_s%d%d" % (b, a), align_bytes=64)
-            nc.vector.quantize_mx(out=w1_c[(b, a)][:].bitcast(E4M3X4), scales=w1_s[(b, a)][:], in_=grouped[:])
+            width = PASS // pieces
+            for c0 in range(0, PASS, width):
+                cols = slice(c0, c0 + width)
+                nc.vector.quantize_mx(
+                    out=w1_c[(b, a)][:, cols].bitcast(E4M3X4),
+                    scales=w1_s[(b, a)][:, cols],
+                    in_=grouped[:, PACK * c0 : PACK * (c0 + width)],
+                )
 
         acc = {}
 
-        def first_product(b, half, a):
+        def first_product(b, t, half, a):
             cols = slice(half * BANK, (half + 1) * BANK)
-            for t in range(PACK):
-                if a == 0:
-                    acc[(b, half, t)] = psum.tile([P, BANK], F32, name="acc%d%d%d" % (b, half, t), tag="bank%d" % (half * PACK + t))
-                nc.tensor.matmul_mx(
-                    out=acc[(b, half, t)][:],
-                    lhsT=w1_c[(b, a)][:, t * P : (t + 1) * P].bitcast(E4M3X4),
-                    lhsT_scale=w1_s[(b, a)][:, t * P : (t + 1) * P],
-                    rhs=v_w[a][:, cols].bitcast(E4M3X4),
-                    rhs_scale=v_s[4 * a : P, cols],
-                    start=(a == 0),
-                    stop=(a == K_PASSES - 1),
-                )
+            if a == 0:
+                acc[(b, t, half)] = psum.tile([P, BANK], F32, name="acc%d%d%d" % (b, t, half), tag="bank%d" % (t * HALVES + half))
+            nc.tensor.matmul_mx(
+                out=acc[(b, t, half)][:],
+                lhsT=w1_c[(b, a)][:, t * P : (t + 1) * P].bitcast(E4M3X4),
+                lhsT_scale=w1_s[(b, a)][:, t * P : (t + 1) * P],
+                rhs=v_w[a][:, cols].bitcast(E4M3X4),
+                rhs_scale=v_s[4 * a : P, cols],
+                start=(a == 0),
+                stop=(a == last),
+            )
 
-        h_rows = {}
+        def first_pass(b, a):
+            for half in range(HALVES):
+                for t in range(PACK):
+                    first_product(b, t, half, a)
+
+        h_rows = [ring.tile([P, 2, S, 2], BF16, name="h_rows%d" % b, tag="h_rows") for b in range(H_PASSES)]
         h_il = {}
         h_c = {}
         h_s = {}
 
-        def distance(b, half, t):
-            if t == 0:
-                h_rows[(b, half)] = ring.tile([P, PACK, BANK], BF16, name="h_rows%d%d" % (b, half), tag="h_rows")
-            d = tgt_sb[(b, half)][:, t, :]
-            nc.vector.tensor_tensor(d, acc[(b, half, t)][:], d, ALU.subtract)
-            nc.scalar.activation(h_rows[(b, half)][:, t, :], d, ACT.Abs, scale=gain_sb[:, b, t : t + 1])
-
-        def apply_sign(b, half):
+        def distance(b, half):
+            cols = slice(half * BANK, (half + 1) * BANK)
             for t in range(PACK):
-                row = h_rows[(b, half)][:, t, :]
-                nc.vector.tensor_scalar(row, row, gain_sign[:, b, t : t + 1], None, ALU.mult)
+                d = tgt_sb[(b, t, half)]
+                nc.vector.tensor_tensor(d, acc[(b, t, half)][:], d, ALU.subtract)
+                nc.scalar.activation(h_rows[b][:, t // 2, cols, t % 2], d, ACT.Abs, scale=gain_sb[:, b, t : t + 1])
 
-        def interleave_h(b, half, vector_share):
-            tile = ring.tile([P, PACK * BANK], BF16, name="h_il%d%d" % (b, half), tag="h_il", align_bytes=64)
-            dst = tile[:].rearrange("p (c i t) -> p c t i", i=4, t=PACK)
-            src = h_rows[(b, half)][:].rearrange("p t (c i) -> p c t i", i=4)
-            if vector_share > 0:
-                nc.vector.tensor_copy(out=dst[:, :vector_share], in_=src[:, :vector_share])
-            if vector_share < P:
-                nc.scalar.copy(out=dst[:, vector_share:], in_=src[:, vector_share:])
+        def interleave_h(b, half):
+            tile = ring.tile([P, PACK * BANK], BF16, name="h_il%d%d" % (b, half), tag="h_il", bufs=1, align_bytes=64)
+            src = h_rows[b][:, :, half * BANK : (half + 1) * BANK, :].rearrange("p u j e -> p j u e")
+            sign = gain_sign[:, b * PACK : (b + 1) * PACK].rearrange("p (u e) -> p u e", e=2)
+            nc.vector.tensor_tensor(
+                tile[:].rearrange("p (j u e) -> p j u e", u=2, e=2),
+                src,
+                sign.unsqueeze(1).to_broadcast([P, BANK, 2, 2]),
+                ALU.mult,
+            )
             h_il[(b, half)] = tile
 
         def quantize_h(b, half):
@@ -181,33 +202,31 @@ def tile_list_salt_pan_pairs_kernel(
             nc.vector.quantize_mx(out=h_c[(b, half)][:].bitcast(E4M3X4), scales=h_s[(b, half)][:], in_=h_il[(b, half)][:])
 
         e_sb = keep.tile([P, PACK, S], F32, name="e_sb")
-
         e_ps = {}
 
-        def second_product(half, b):
-            for t in range(PACK):
-                if b == 0:
-                    e_ps[(half, t)] = psum.tile([P, BANK], F32, name="e%d%d" % (half, t), tag="bank%d" % (half * PACK + t))
-                nc.tensor.matmul_mx(
-                    out=e_ps[(half, t)][:],
-                    lhsT=w2_c[:, b, 2 * t * P : 2 * (t + 1) * P].bitcast(E2M1X4),
-                    lhsT_scale=w2_s[:, b, t * P : (t + 1) * P],
-                    rhs=h_c[(b, half)][:].bitcast(E4M3X4),
-                    rhs_scale=h_s[(b, half)][:],
-                    start=(b == 0),
-                    stop=(b == H_PASSES - 1),
-                )
-                if b == H_PASSES - 1:
-                    nc.scalar.copy(out=e_sb[:, t, half * BANK : (half + 1) * BANK], in_=e_ps[(half, t)][:])
+        def second_product(t, half, b):
+            if b == 0:
+                e_ps[(t, half)] = psum.tile([P, BANK], F32, name="e%d%d" % (t, half), tag="bank%d" % (t * HALVES + half))
+            nc.tensor.matmul_mx(
+                out=e_ps[(t, half)][:],
+                lhsT=w2_c[:, b, 2 * t * P : 2 * (t + 1) * P].bitcast(E2M1X4),
+                lhsT_scale=w2_s[:, b, t * P : (t + 1) * P],
+                rhs=h_c[(b, half)][:].bitcast(E4M3X4),
+                rhs_scale=h_s[(b, half)][:],
+                start=(b == 0),
+                stop=(b == H_PASSES - 1),
+            )
 
-        for a in range(K_PASSES - 1):
-            grouped = round_w1(0, a, 0)
-            gather_words(a, 0, S)
+        def evacuate(t, half):
+            nc.scalar.copy(out=e_sb[:, t, half * BANK : (half + 1) * BANK], in_=e_ps[(t, half)][:])
+
+        for a in range(last):
+            gather_words(a)
             if a == 0:
                 nc.vector.tensor_copy(v_s[:], tab_s[:].indirect(offs_sb[:]))
-            quantize_w1(0, a, grouped)
-            for half in range(HALVES):
-                first_product(0, half, a)
+            for b in range(H_PASSES):
+                quantize_w1(b, a, round_w1(b, a, 0))
+            first_pass(0, a)
         for b in range(H_PASSES):
             nc.vector.tensor_copy(
                 out=w2_c[:, b, :].rearrange("p (t q e) -> p t q e", t=PACK, e=2),
@@ -217,113 +236,99 @@ def tile_list_salt_pan_pairs_kernel(
             out=w2_s[:].rearrange("p b (t q) -> p b t q", t=PACK),
             in_=w2s_raw[:].rearrange("p b (q t) -> p b t q", t=PACK),
         )
-        last = K_PASSES - 1
-        gather_words(last, 0, S)
-        quantize_w1(0, last, round_w1(0, last, P // 2))
-        first_product(0, 0, last)
-        first_product(0, 1, last)
+        gather_words(last)
+        quantize_w1(0, last, round_w1(0, last, 84), 4)
+        first_pass(0, last)
 
-        for t in range(PACK):
-            distance(0, 0, t)
-        g10 = round_w1(1, 0, 0)
-        apply_sign(0, 0)
-        interleave_h(0, 0, P)
-        distance(0, 1, 0)
+        for half in range(HALVES):
+            distance(0, half)
+            for a in range(last):
+                for t in range(PACK):
+                    first_product(1, t, half, a)
+        quantize_w1(1, last, round_w1(1, last, 128))
+        first_pass(1, last)
+        interleave_h(0, 0)
         quantize_h(0, 0)
-        for t in range(1, PACK):
-            distance(0, 1, t)
-        quantize_w1(1, 0, g10)
-        first_product(1, 0, 0)
-        g11 = round_w1(1, 1, 0)
-        apply_sign(0, 1)
-        interleave_h(0, 1, P)
-        quantize_w1(1, 1, g11)
-        first_product(1, 1, 0)
-        first_product(1, 0, 1)
-        first_product(1, 1, 1)
-        g12 = round_w1(1, 2, P // 2)
+        distance(1, 0)
+        interleave_h(0, 1)
         quantize_h(0, 1)
-        quantize_w1(1, 2, g12)
-        first_product(1, 0, 2)
-        first_product(1, 1, 2)
-        for t in range(PACK):
-            distance(1, 0, t)
-        second_product(0, 0)
-        distance(1, 1, 0)
-        apply_sign(1, 0)
-        interleave_h(1, 0, 0)
-        for t in range(1, PACK):
-            distance(1, 1, t)
-        quantize_h(1, 0)
-        second_product(0, 1)
-        second_product(1, 0)
-        apply_sign(1, 1)
-        interleave_h(1, 1, 88)
-        quantize_h(1, 1)
-        second_product(1, 1)
+        distance(1, 1)
+        for half in range(HALVES):
+            for t in range(PACK):
+                second_product(t, half, 0)
+        for half in range(HALVES):
+            interleave_h(1, half)
+            quantize_h(1, half)
+            for t in range(PACK):
+                second_product(t, half, 1)
+                evacuate(t, half)
 
         y_c = keep.tile([P, M], U32, name="y_c", align_bytes=64)
         y_s = keep.tile([P, M], U8, name="y_s", align_bytes=64)
         out_rows = out_0.rearrange("(p t) m -> p t m", t=PACK)
         out_words = out_1[0].rearrange("p m i -> p (m i)").bitcast(I32)
-        state = {}
+        y = keep.tile([P, PACK, M], F32, name="y")
+        y_il = keep.tile([P, PACK * M], BF16, name="y_il", align_bytes=64)
+        pair = {}
+        turns = {}
 
-        def pick(c, m0, w):
-            pair = stage.tile([P, 2, PACK, w], F32, name="pair%d" % c, tag="stage")
-            for t in range(PACK):
-                for side in range(2):
-                    nc.vector.tensor_copy(
-                        pair[:, side, t, :], e_sb[:, t, :].indirect(pos_sb[side][:, m0 // 16 : (m0 + w) // 16])
-                    )
-            state[c] = pair
+        def pick(t, m0, m1):
+            if m0 == 0:
+                pair[t] = ring.tile([P, 2, M], F32, name="pair%d" % t, tag="tgt", bufs=4)
+                turns[t] = ring.tile([P, M], I32, name="turns%d" % t, tag="narrow")
+            for side in range(2):
+                nc.vector.tensor_copy(pair[t][:, side, m0:m1], e_sb[:, t, :].indirect(pos_sb[side][:, m0 // 16 : m1 // 16]))
 
-        def reduce_angle(c, m0, w):
-            pair = state[c]
-            low = pair[:, 0].rearrange("p t m -> p (t m)")
-            frac = pair[:, 1].rearrange("p t m -> p (t m)")
-            turns = tgt.tile([P, PACK * w], I32, name="turns%d" % c, tag="tgt")
-            y = ring.tile([P, PACK, w], F32, name="y%d" % c, tag="y", bufs=3)
+        def reduce_angle(t, m0, m1):
+            low, frac, whole = pair[t][:, 0, m0:m1], pair[t][:, 1, m0:m1], turns[t][:, m0:m1]
             nc.vector.tensor_tensor(low, low, frac, ALU.min)
-            nc.vector.tensor_scalar(turns[:], low, 0.5 / math.pi, None, ALU.mult)
-            nc.vector.scalar_tensor_tensor(frac, low, 0.5 / math.pi, turns[:], ALU.mult, ALU.subtract)
-            for t in range(PACK):
-                nc.scalar.activation(y[:, t, :], pair[:, 0, t, :], ACT.Copy, scale=sluice_sb[:, t : t + 1])
+            nc.vector.tensor_scalar(whole, low, 0.5 / math.pi, None, ALU.mult)
+            nc.vector.scalar_tensor_tensor(frac, low, 0.5 / math.pi, whole, ALU.mult, ALU.subtract)
             nc.scalar.activation(frac, frac, ACT.Sin, scale=2.0 * math.pi)
-            state[(c, "y")] = y
 
-        def finish(c, m0, w):
-            pair = state[c]
-            y = state[(c, "y")]
-            for t in range(PACK):
-                nc.vector.scalar_tensor_tensor(
-                    y[:, t, :], pair[:, 1, t, :], sluice_sb[:, t : t + 1], y[:, t, :], ALU.mult, ALU.add
-                )
-            nc.sync.dma_start(out=out_rows[:, :, m0 : m0 + w], in_=y[:])
-            y_il = ring.tile([P, PACK * w], BF16, name="y_il%d" % c, tag="y_il", align_bytes=64)
-            dst = y_il[:].rearrange("p (c i t) -> p c t i", i=4, t=PACK)
-            src = y[:].rearrange("p t (c i) -> p c t i", i=4)
-            if c < len(PAIR_CHUNKS) - 1:
-                nc.scalar.copy(out=dst, in_=src)
+        def scale_low(t, m0, m1):
+            nc.scalar.activation(y[:, t, m0:m1], pair[t][:, 0, m0:m1], ACT.Copy, scale=sluice_sb[:, t : t + 1])
+
+        def add_on_vector(t, m0, m1):
+            nc.vector.scalar_tensor_tensor(
+                y[:, t, m0:m1], pair[t][:, 1, m0:m1], sluice_sb[:, t : t + 1], y[:, t, m0:m1], ALU.mult, ALU.add
+            )
+            if m1 == M:
+                nc.sync.dma_start(out=out_rows[:, t, :], in_=y[:, t, :])
+
+        def interleave_y(m0, m1):
+            dst = y_il[:, PACK * m0 : PACK * m1].rearrange("p (c i t) -> p c t i", i=4, t=PACK)
+            nc.vector.tensor_copy(out=dst, in_=y[:, :, m0:m1].rearrange("p t (c i) -> p c t i", i=4))
+
+        def planes(m0, m1):
+            nc.vector.quantize_mx(
+                out=y_c[:, m0:m1].bitcast(E4M3X4), scales=y_s[:, m0:m1], in_=y_il[:, PACK * m0 : PACK * m1]
+            )
+            if m1 == M:
+                nc.sync.dma_start(out=out_words, in_=y_c[:].bitcast(I32))
+
+        final = PACK - 1
+        pick(0, 0, M)
+        for t in range(final):
+            if t + 1 < final:
+                pick(t + 1, 0, M)
             else:
-                nc.vector.tensor_copy(out=dst, in_=src)
-            state[(c, "il")] = y_il
+                pick(final, 0, M // 2)
+            reduce_angle(t, 0, M)
+            scale_low(t, 0, M)
+            add_on_vector(t, 0, M)
+        pick(final, M // 2, M)
+        parts = ((0, M // 2), (M // 2, M))
+        for part in parts:
+            reduce_angle(final, *part)
+            scale_low(final, *part)
+        for part in parts:
+            add_on_vector(final, *part)
+        for part in parts:
+            interleave_y(*part)
+        for part in parts:
+            planes(*part)
 
-        def planes(c, m0, w):
-            cols = slice(m0, m0 + w)
-            nc.vector.quantize_mx(out=y_c[:, cols].bitcast(E4M3X4), scales=y_s[:, cols], in_=state[(c, "il")][:])
-            nc.sync.dma_start(out=out_words[:, cols], in_=y_c[:, cols].bitcast(I32))
-
-        starts = [sum(PAIR_CHUNKS[:c]) for c in range(len(PAIR_CHUNKS))]
-        chunks = [(c, starts[c], PAIR_CHUNKS[c]) for c in range(len(PAIR_CHUNKS))]
-        for step in range(len(chunks) + 2):
-            if step < len(chunks):
-                pick(*chunks[step])
-            if 2 <= step:
-                planes(*chunks[step - 2])
-            if step < len(chunks):
-                reduce_angle(*chunks[step])
-            if 1 <= step <= len(chunks):
-                finish(*chunks[step - 1])
         for q in range(4):
             queue = nc.scalar if q % 2 else nc.sync
             queue.dma_start(

@@ -24,6 +24,7 @@ K_PASSES = K // PASS
 H_PASSES = H // PASS
 BANK = 512
 HALVES = S // BANK
+ROUNDING = 1.5 * 2.0**23
 
 
 def tile_list_salt_pan_pairs_kernel(
@@ -91,17 +92,17 @@ def tile_list_salt_pan_pairs_kernel(
                 out=tab_s[32 * q : 32 * q + 4 * K_PASSES, :].bitcast(I32),
                 in_=tab_scales[:, 4 * q : 4 * q + 4, :].bitcast(I32),
             )
-        load_w1_rows(0)
-        load_table(1)
-        load_w1_rows(1)
         nc.sync.dma_start(out=w2_raw[:].bitcast(I32), in_=w2_words.rearrange("a p b -> p a b").bitcast(I32))
         for q in range(4):
             nc.sync.dma_start(
                 out=w2s_raw[32 * q : 32 * q + 4, :, :].bitcast(I32),
                 in_=w2_scales[:, 4 * q : 4 * q + 4, :].rearrange("a r c -> r a c").bitcast(I32),
             )
-        load_table(2)
+        load_w1_rows(0)
+        load_table(1)
+        load_w1_rows(1)
         load_w1_block(0, last, "narrow", (0, PASS))
+        load_table(2)
         load_target(0, 0)
         load_target(0, 1)
         load_w1_block(1, last, "narrow", (0, PASS))
@@ -122,8 +123,8 @@ def tile_list_salt_pan_pairs_kernel(
         w1_c = {}
         w1_s = {}
 
-        def gather_words(a):
-            nc.vector.tensor_copy(v_w[a][:], tab_w[a][:].bitcast(U32).indirect(offs_sb[:]))
+        def gather_words(a, j0=0, j1=S):
+            nc.vector.tensor_copy(v_w[a][:, j0:j1], tab_w[a][:].bitcast(U32).indirect(offs_sb[:, j0 // 16 : j1 // 16]))
 
         def shared_copy(dst, src, vector_share):
             n = dst.shape[1]
@@ -177,44 +178,56 @@ def tile_list_salt_pan_pairs_kernel(
         h_c = {}
         h_s = {}
 
-        def distance(b, half):
-            cols = slice(half * BANK, (half + 1) * BANK)
-            for t in range(PACK):
-                d = tgt_sb[(b, t, half)]
-                nc.vector.tensor_tensor(d, acc[(b, t, half)][:], d, ALU.subtract)
-                nc.scalar.activation(h_rows[b][:, t // 2, cols, t % 2], d, ACT.Abs, scale=gain_sb[:, b, t : t + 1])
+        def subtract_target(b, t, half):
+            d = tgt_sb[(b, t, half)]
+            nc.vector.tensor_tensor(d, acc[(b, t, half)][:], d, ALU.subtract)
 
-        def interleave_h(b, half):
-            tile = ring.tile([P, PACK * BANK], BF16, name="h_il%d%d" % (b, half), tag="h_il", bufs=1, align_bytes=64)
-            src = h_rows[b][:, :, half * BANK : (half + 1) * BANK, :].rearrange("p u j e -> p j u e")
+        def magnitude(b, t, half, c0, c1):
+            dst = h_rows[b][:, t // 2, half * BANK + c0 : half * BANK + c1, t % 2]
+            nc.scalar.activation(dst, tgt_sb[(b, t, half)][:, c0:c1], ACT.Abs, scale=gain_sb[:, b, t : t + 1])
+
+        def distance(b, half, width=BANK):
+            for t in range(PACK):
+                subtract_target(b, t, half)
+                magnitude(b, t, half, 0, width)
+            for c0 in range(width, BANK, width):
+                for t in range(PACK):
+                    magnitude(b, t, half, c0, c0 + width)
+
+        def interleave_h(b, half, c0=0, c1=BANK):
+            tile = ring.tile([P, PACK * (c1 - c0)], BF16, name="h_il%d%d%d" % (b, half, c0), tag="h_il", bufs=1, align_bytes=64)
+            src = h_rows[b][:, :, half * BANK + c0 : half * BANK + c1, :].rearrange("p u j e -> p j u e")
             sign = gain_sign[:, b * PACK : (b + 1) * PACK].rearrange("p (u e) -> p u e", e=2)
             nc.vector.tensor_tensor(
                 tile[:].rearrange("p (j u e) -> p j u e", u=2, e=2),
                 src,
-                sign.unsqueeze(1).to_broadcast([P, BANK, 2, 2]),
+                sign.unsqueeze(1).to_broadcast([P, c1 - c0, 2, 2]),
                 ALU.mult,
             )
-            h_il[(b, half)] = tile
+            h_il[(b, half, c0)] = tile
 
-        def quantize_h(b, half):
-            h_c[(b, half)] = keep.tile([P, BANK], U32, name="h_c%d%d" % (b, half), align_bytes=64)
-            h_s[(b, half)] = keep.tile([P, BANK], U8, name="h_s%d%d" % (b, half), align_bytes=64)
-            nc.vector.quantize_mx(out=h_c[(b, half)][:].bitcast(E4M3X4), scales=h_s[(b, half)][:], in_=h_il[(b, half)][:])
+        def quantize_h(b, half, c0=0, c1=BANK):
+            if c0 == 0:
+                h_c[(b, half)] = keep.tile([P, BANK], U32, name="h_c%d%d" % (b, half), align_bytes=64)
+                h_s[(b, half)] = keep.tile([P, BANK], U8, name="h_s%d%d" % (b, half), align_bytes=64)
+            nc.vector.quantize_mx(
+                out=h_c[(b, half)][:, c0:c1].bitcast(E4M3X4), scales=h_s[(b, half)][:, c0:c1], in_=h_il[(b, half, c0)][:]
+            )
 
         e_sb = keep.tile([P, PACK, S], F32, name="e_sb")
         e_ps = {}
 
-        def second_product(t, half, b):
+        def second_product(t, half, b, c0=0, c1=BANK):
             if b == 0:
                 e_ps[(t, half)] = psum.tile([P, BANK], F32, name="e%d%d" % (t, half), tag="bank%d" % (t * HALVES + half))
             nc.tensor.matmul_mx(
-                out=e_ps[(t, half)][:],
+                out=e_ps[(t, half)][:, c0:c1],
                 lhsT=w2_c[:, b, 2 * t * P : 2 * (t + 1) * P].bitcast(E2M1X4),
                 lhsT_scale=w2_s[:, b, t * P : (t + 1) * P],
-                rhs=h_c[(b, half)][:].bitcast(E4M3X4),
-                rhs_scale=h_s[(b, half)][:],
+                rhs=h_c[(b, half)][:, c0:c1].bitcast(E4M3X4),
+                rhs_scale=h_s[(b, half)][:, c0:c1],
                 start=(b == 0),
-                stop=(b == H_PASSES - 1),
+                stop=(b == H_PASSES - 1 and c1 == BANK),
             )
 
         def evacuate(t, half):
@@ -236,32 +249,46 @@ def tile_list_salt_pan_pairs_kernel(
             out=w2_s[:].rearrange("p b (t q) -> p b t q", t=PACK),
             in_=w2s_raw[:].rearrange("p b (q t) -> p b t q", t=PACK),
         )
-        gather_words(last)
-        quantize_w1(0, last, round_w1(0, last, 84), 4)
-        first_pass(0, last)
-
+        quantize_w1(0, last, round_w1(0, last, 128))
         for half in range(HALVES):
-            distance(0, half)
-            for a in range(last):
-                for t in range(PACK):
-                    first_product(1, t, half, a)
-        quantize_w1(1, last, round_w1(1, last, 128))
+            gather_words(last, half * BANK, (half + 1) * BANK)
+            for t in range(PACK):
+                first_product(0, t, half, last)
+
+        distance(0, 0)
+        for a in range(last):
+            for t in range(PACK):
+                first_product(1, t, 0, a)
+        grouped = round_w1(1, last, 64)
+        distance(0, 1)
+        for a in range(last):
+            for t in range(PACK):
+                first_product(1, t, 1, a)
+
+        quantize_w1(1, last, grouped, 4)
         first_pass(1, last)
         interleave_h(0, 0)
         quantize_h(0, 0)
         distance(1, 0)
         interleave_h(0, 1)
         quantize_h(0, 1)
-        distance(1, 1)
+        distance(1, 1, 512)
         for half in range(HALVES):
             for t in range(PACK):
                 second_product(t, half, 0)
-        for half in range(HALVES):
-            interleave_h(1, half)
-            quantize_h(1, half)
+        interleave_h(1, 0)
+        quantize_h(1, 0)
+        for t in range(PACK):
+            second_product(t, 0, 1)
+            evacuate(t, 0)
+        for c0 in range(0, BANK, 512):
+            interleave_h(1, 1, c0, c0 + 512)
+            quantize_h(1, 1, c0, c0 + 512)
             for t in range(PACK):
-                second_product(t, half, 1)
-                evacuate(t, half)
+                for n0 in range(c0, c0 + 512, 512):
+                    second_product(t, 1, 1, n0, n0 + 512)
+                if c0 + 512 == BANK:
+                    evacuate(t, 1)
 
         y_c = keep.tile([P, M], U32, name="y_c", align_bytes=64)
         y_s = keep.tile([P, M], U8, name="y_s", align_bytes=64)
@@ -282,8 +309,13 @@ def tile_list_salt_pan_pairs_kernel(
         def reduce_angle(t, m0, m1):
             low, frac, whole = pair[t][:, 0, m0:m1], pair[t][:, 1, m0:m1], turns[t][:, m0:m1]
             nc.vector.tensor_tensor(low, low, frac, ALU.min)
-            nc.vector.tensor_scalar(whole, low, 0.5 / math.pi, None, ALU.mult)
-            nc.vector.scalar_tensor_tensor(frac, low, 0.5 / math.pi, whole, ALU.mult, ALU.subtract)
+            if t < 3:
+                nc.scalar.activation(whole.bitcast(U32), low, ACT.Copy, scale=0.5 / math.pi, bias=ROUNDING)
+                nc.scalar.activation(frac, whole.bitcast(U32), ACT.Copy, scale=1.0, bias=-ROUNDING)
+                nc.vector.scalar_tensor_tensor(frac, low, 0.5 / math.pi, frac, ALU.mult, ALU.subtract)
+            else:
+                nc.vector.tensor_scalar(whole, low, 0.5 / math.pi, None, ALU.mult)
+                nc.vector.scalar_tensor_tensor(frac, low, 0.5 / math.pi, whole, ALU.mult, ALU.subtract)
             nc.scalar.activation(frac, frac, ACT.Sin, scale=2.0 * math.pi)
 
         def scale_low(t, m0, m1):
@@ -293,41 +325,39 @@ def tile_list_salt_pan_pairs_kernel(
             nc.vector.scalar_tensor_tensor(
                 y[:, t, m0:m1], pair[t][:, 1, m0:m1], sluice_sb[:, t : t + 1], y[:, t, m0:m1], ALU.mult, ALU.add
             )
-            if m1 == M:
-                nc.sync.dma_start(out=out_rows[:, t, :], in_=y[:, t, :])
+            nc.sync.dma_start(out=out_rows[:, t, m0:m1], in_=y[:, t, m0:m1])
 
-        def interleave_y(m0, m1):
+        def interleave_y(m0, m1, vector_share):
             dst = y_il[:, PACK * m0 : PACK * m1].rearrange("p (c i t) -> p c t i", i=4, t=PACK)
-            nc.vector.tensor_copy(out=dst, in_=y[:, :, m0:m1].rearrange("p t (c i) -> p c t i", i=4))
+            shared_copy(dst, y[:, :, m0:m1].rearrange("p t (c i) -> p c t i", i=4), vector_share)
 
         def planes(m0, m1):
             nc.vector.quantize_mx(
                 out=y_c[:, m0:m1].bitcast(E4M3X4), scales=y_s[:, m0:m1], in_=y_il[:, PACK * m0 : PACK * m1]
             )
-            if m1 == M:
-                nc.sync.dma_start(out=out_words, in_=y_c[:].bitcast(I32))
+
+        def store_words(m0, m1):
+            nc.sync.dma_start(out=out_words[:, m0:m1], in_=y_c[:, m0:m1].bitcast(I32))
 
         final = PACK - 1
-        pick(0, 0, M)
+        parts = ((0, 256), (256, M))
         for t in range(final):
-            if t + 1 < final:
-                pick(t + 1, 0, M)
-            else:
-                pick(final, 0, M // 2)
+            pick(t, 0, M)
             reduce_angle(t, 0, M)
             scale_low(t, 0, M)
             add_on_vector(t, 0, M)
-        pick(final, M // 2, M)
-        parts = ((0, M // 2), (M // 2, M))
         for part in parts:
+            pick(final, *part)
             reduce_angle(final, *part)
             scale_low(final, *part)
         for part in parts:
             add_on_vector(final, *part)
-        for part in parts:
-            interleave_y(*part)
-        for part in parts:
-            planes(*part)
+        interleave_y(*parts[0], 0)
+        interleave_y(*parts[1], (M - 256) // 4)
+        for m0, m1 in parts:
+            for c0 in range(m0, m1, 256):
+                planes(c0, min(m1, c0 + 256))
+            store_words(m0, m1)
 
         for q in range(4):
             queue = nc.scalar if q % 2 else nc.sync

@@ -2,6 +2,7 @@ import math
 from contextlib import ExitStack
 
 import concourse.mybir as mybir
+from concourse.masks import make_identity
 
 K, H, N, T, S, M = 1536, 1024, 512, 4096, 1024, 512
 FLOPS = 2 * K * H * S + 2 * H * N * S
@@ -22,8 +23,12 @@ PACK = 4
 PASS = P * PACK
 K_PASSES = K // PASS
 H_PASSES = H // PASS
+LAST_K = K_PASSES - 1
 BANK = 512
 HALVES = S // BANK
+QUADRANTS = 4
+LIST_ROWS = 16
+TURN = 2.0 * math.pi
 ROUNDING = 1.5 * 2.0**23
 
 
@@ -36,8 +41,11 @@ def tile_list_salt_pan_pairs_kernel(
         ring = ctx.enter_context(tc.tile_pool(name="ring", bufs=2))
         psum = ctx.enter_context(tc.psum_pool(name="psum", bufs=1))
 
-        offs_sb = keep.tile([P, S // 16], U16, name="offs_sb")
-        pos_sb = [keep.tile([P, M // 16], U16, name="pos1_sb"), keep.tile([P, M // 16], U16, name="pos2_sb")]
+        def bank(name, t, i):
+            return psum.tile([P, BANK], F32, name=name, tag="bank%d" % (HALVES * t + i))
+
+        offs_sb = keep.tile([P, S // LIST_ROWS], U16, name="offs_sb")
+        pos_sb = [keep.tile([P, M // LIST_ROWS], U16, name="pos%d_sb" % side) for side in (1, 2)]
         tab_w = [keep.tile([P, T], I32, name="tab_w%d" % a) for a in range(K_PASSES)]
         tab_s = keep.tile([P, T], U8, name="tab_s")
         w2_raw = keep.tile([P, H_PASSES, 2 * N], U8, name="w2_raw")
@@ -48,11 +56,11 @@ def tile_list_salt_pan_pairs_kernel(
         nc.vector.memset(tab_s[:].bitcast(I32), 0)
         nc.vector.memset(w2s_raw[:].bitcast(I32), 0)
         nc.sync.dma_start(offs_sb[:], offs)
-        nc.scalar.dma_start(out=gain_sb[:], in_=gain.rearrange("(a p t) -> p a t", a=H_PASSES, t=PACK))
+        nc.scalar.dma_start(out=gain_sb[:], in_=gain.rearrange("(b p t) -> p b t", b=H_PASSES, t=PACK))
         nc.scalar.dma_start(out=sluice_sb[:], in_=sluice.rearrange("(p t) -> p t", t=PACK))
 
         w1_raw = {}
-        tgt_sb = {}
+        target_sb = {}
 
         def load_table(a):
             nc.sync.dma_start(out=tab_w[a][:], in_=tab_words[a].rearrange("p t i -> p (t i)").bitcast(I32))
@@ -63,87 +71,75 @@ def tile_list_salt_pan_pairs_kernel(
             for b in range(H_PASSES):
                 w1_raw[(b, a)] = raw[:, :, b * PASS : (b + 1) * PASS]
 
-        def load_w1_block(b, a, tag, cuts):
-            raw = ring.tile([P, PACK, PASS], F32, name="w1_raw%d%d" % (b, a), tag=tag)
+        def load_w1_block(b, a):
+            raw = ring.tile([P, PACK, PASS], F32, name="w1_raw%d%d" % (b, a), tag="narrow")
             rows = w1[a * PASS : (a + 1) * PASS, b * PASS : (b + 1) * PASS]
-            for c0, c1 in zip(cuts, cuts[1:]):
-                nc.sync.dma_start(out=raw[:, :, c0:c1], in_=rows[:, c0:c1].rearrange("(p i) c -> p i c", i=PACK))
+            nc.sync.dma_start(out=raw[:], in_=rows.rearrange("(p i) c -> p i c", i=PACK))
             w1_raw[(b, a)] = raw[:]
 
         def load_target(b, u):
-            tile = ring.tile([P, 2, S], F32, name="pairT%d%d" % (b, u), tag="tgt", bufs=4)
+            tile = ring.tile([P, 2, S], F32, name="target%d%d" % (b, u), tag="rows", bufs=4)
             rows = target[b * PASS : (b + 1) * PASS, :].rearrange("(p t) j -> p t j", t=PACK)
             nc.sync.dma_start(out=tile[:], in_=rows[:, 2 * u : 2 * u + 2, :])
-            for t in range(2):
+            for e in range(2):
                 for half in range(HALVES):
-                    tgt_sb[(b, 2 * u + t, half)] = tile[:, t, half * BANK : (half + 1) * BANK]
+                    target_sb[(b, 2 * u + e, half)] = tile[:, e, half * BANK : (half + 1) * BANK]
 
-        def load_target_half(b, half):
-            tile = ring.tile([P, PACK, BANK], F32, name="tgt%d%d" % (b, half), tag="tgt", bufs=4)
-            rows = target[b * PASS : (b + 1) * PASS, half * BANK : (half + 1) * BANK]
-            nc.sync.dma_start(out=tile[:], in_=rows.rearrange("(p t) j -> p t j", t=PACK))
-            for t in range(PACK):
-                tgt_sb[(b, t, half)] = tile[:, t, :]
-
-        last = K_PASSES - 1
         load_table(0)
-        for q in range(4):
+        for q in range(QUADRANTS):
             nc.gpsimd.dma_start(
                 out=tab_s[32 * q : 32 * q + 4 * K_PASSES, :].bitcast(I32),
                 in_=tab_scales[:, 4 * q : 4 * q + 4, :].bitcast(I32),
             )
-        nc.sync.dma_start(out=w2_raw[:].bitcast(I32), in_=w2_words.rearrange("a p b -> p a b").bitcast(I32))
-        for q in range(4):
+        nc.sync.dma_start(out=w2_raw[:].bitcast(I32), in_=w2_words.rearrange("b p c -> p b c").bitcast(I32))
+        for q in range(QUADRANTS):
             nc.sync.dma_start(
                 out=w2s_raw[32 * q : 32 * q + 4, :, :].bitcast(I32),
-                in_=w2_scales[:, 4 * q : 4 * q + 4, :].rearrange("a r c -> r a c").bitcast(I32),
+                in_=w2_scales[:, 4 * q : 4 * q + 4, :].rearrange("b r c -> r b c").bitcast(I32),
             )
-        load_w1_rows(0)
-        load_table(1)
-        load_w1_rows(1)
-        load_w1_block(0, last, "narrow", (0, PASS))
-        load_table(2)
+        for a in range(LAST_K):
+            load_w1_rows(a)
+            if a + 1 < LAST_K:
+                load_table(a + 1)
+        load_w1_block(0, LAST_K)
+        load_table(LAST_K)
         load_target(0, 0)
         load_target(0, 1)
-        load_w1_block(1, last, "narrow", (0, PASS))
+        load_w1_block(1, LAST_K)
         load_target(1, 0)
         load_target(1, 1)
         nc.sync.dma_start(pos_sb[0][:], pos1)
         nc.sync.dma_start(pos_sb[1][:], pos2)
 
-        w2_c = keep.tile([P, H_PASSES, 2 * N], U8, name="w2_c", align_bytes=64)
-        w2_s = keep.tile([P, H_PASSES, N], U8, name="w2_s", align_bytes=64)
         gain_half = keep.tile([P, H_PASSES * PACK], F32, name="gain_half")
         gain_sign = keep.tile([P, H_PASSES * PACK], BF16, name="gain_sign")
         nc.vector.tensor_scalar(gain_half[:], gain_sb[:].rearrange("p b t -> p (b t)"), 0.0, -0.5, ALU.is_ge, ALU.add)
         nc.scalar.activation(gain_sign[:], gain_half[:], ACT.Sin, scale=math.pi)
+        identity = keep.tile([P, P], F32, name="identity")
+        make_identity(nc, identity[:])
+        sluice_turn = keep.tile([P, PACK], F32, name="sluice_turn")
+        nc.vector.tensor_scalar(sluice_turn[:], sluice_sb[:], TURN, None, ALU.mult)
 
         v_w = [keep.tile([P, S], U32, name="v_w%d" % a, align_bytes=64) for a in range(K_PASSES)]
-        v_s = keep.tile([P, S], U8, name="v_s", align_bytes=64)
         w1_c = {}
         w1_s = {}
+        acc = {}
 
-        def gather_words(a, j0=0, j1=S):
-            nc.vector.tensor_copy(v_w[a][:, j0:j1], tab_w[a][:].bitcast(U32).indirect(offs_sb[:, j0 // 16 : j1 // 16]))
+        def gather_words(a, j0, j1):
+            offsets = offs_sb[:, j0 // LIST_ROWS : j1 // LIST_ROWS]
+            nc.vector.tensor_copy(v_w[a][:, j0:j1], tab_w[a][:].bitcast(U32).indirect(offsets))
 
-        def shared_copy(dst, src, vector_share):
-            n = dst.shape[1]
-            if vector_share < n:
-                nc.scalar.copy(out=dst[:, vector_share:], in_=src[:, vector_share:])
-            if vector_share > 0:
-                nc.vector.tensor_copy(out=dst[:, :vector_share], in_=src[:, :vector_share])
-
-        def round_w1(b, a, vector_share):
-            grouped = ring.tile([P, PACK * PASS], BF16, name="w1_bf%d%d" % (b, a), tag="w1_bf", align_bytes=64)
-            dst = grouped[:].rearrange("p (t m i) -> p m i t", t=PACK, i=PACK)
-            src = w1_raw[(b, a)].rearrange("p i (m t) -> p m i t", t=PACK)
-            shared_copy(dst, src, vector_share)
+        def round_w1(b, a, copy, tag="w1_bf", bufs=2):
+            grouped = ring.tile([P, PACK * PASS], BF16, name="w1_bf%d%d" % (b, a), tag=tag, bufs=bufs, align_bytes=64)
+            copy(
+                out=grouped[:].rearrange("p (t m i) -> p m i t", t=PACK, i=PACK),
+                in_=w1_raw[(b, a)].rearrange("p i (m t) -> p m i t", t=PACK),
+            )
             return grouped
 
-        def quantize_w1(b, a, grouped, pieces=1):
+        def quantize_w1(b, a, grouped, width=PASS):
             w1_c[(b, a)] = keep.tile([P, PASS], U32, name="w1_c%d%d" % (b, a), align_bytes=64)
             w1_s[(b, a)] = keep.tile([P, PASS], U8, name="w1_s%d%d" % (b, a), align_bytes=64)
-            width = PASS // pieces
             for c0 in range(0, PASS, width):
                 cols = slice(c0, c0 + width)
                 nc.vector.quantize_mx(
@@ -152,214 +148,190 @@ def tile_list_salt_pan_pairs_kernel(
                     in_=grouped[:, PACK * c0 : PACK * (c0 + width)],
                 )
 
-        acc = {}
-
-        def first_product(b, t, half, a):
+        def first_product(v_s, b, half, a):
             cols = slice(half * BANK, (half + 1) * BANK)
-            if a == 0:
-                acc[(b, t, half)] = psum.tile([P, BANK], F32, name="acc%d%d%d" % (b, t, half), tag="bank%d" % (t * HALVES + half))
-            nc.tensor.matmul_mx(
-                out=acc[(b, t, half)][:],
-                lhsT=w1_c[(b, a)][:, t * P : (t + 1) * P].bitcast(E4M3X4),
-                lhsT_scale=w1_s[(b, a)][:, t * P : (t + 1) * P],
-                rhs=v_w[a][:, cols].bitcast(E4M3X4),
-                rhs_scale=v_s[4 * a : P, cols],
-                start=(a == 0),
-                stop=(a == last),
-            )
-
-        def first_pass(b, a):
-            for half in range(HALVES):
-                for t in range(PACK):
-                    first_product(b, t, half, a)
-
-        h_rows = [ring.tile([P, 2, S, 2], BF16, name="h_rows%d" % b, tag="h_rows") for b in range(H_PASSES)]
-        h_il = {}
-        h_c = {}
-        h_s = {}
-
-        def subtract_target(b, t, half):
-            d = tgt_sb[(b, t, half)]
-            nc.vector.tensor_tensor(d, acc[(b, t, half)][:], d, ALU.subtract)
-
-        def magnitude(b, t, half, c0, c1):
-            dst = h_rows[b][:, t // 2, half * BANK + c0 : half * BANK + c1, t % 2]
-            nc.scalar.activation(dst, tgt_sb[(b, t, half)][:, c0:c1], ACT.Abs, scale=gain_sb[:, b, t : t + 1])
-
-        def distance(b, half, width=BANK):
             for t in range(PACK):
-                subtract_target(b, t, half)
-                magnitude(b, t, half, 0, width)
-            for c0 in range(width, BANK, width):
-                for t in range(PACK):
-                    magnitude(b, t, half, c0, c0 + width)
+                if a == 0:
+                    acc[(b, t, half)] = bank("acc%d%d%d" % (b, t, half), t, half)
+                nc.tensor.matmul_mx(
+                    out=acc[(b, t, half)][:],
+                    lhsT=w1_c[(b, a)][:, t * P : (t + 1) * P].bitcast(E4M3X4),
+                    lhsT_scale=w1_s[(b, a)][:, t * P : (t + 1) * P],
+                    rhs=v_w[a][:, cols].bitcast(E4M3X4),
+                    rhs_scale=v_s[4 * a : P, cols],
+                    start=(a == 0),
+                    stop=(a == LAST_K),
+                )
 
-        def interleave_h(b, half, c0=0, c1=BANK):
-            tile = ring.tile([P, PACK * (c1 - c0)], BF16, name="h_il%d%d%d" % (b, half, c0), tag="h_il", bufs=1, align_bytes=64)
-            src = h_rows[b][:, :, half * BANK + c0 : half * BANK + c1, :].rearrange("p u j e -> p j u e")
-            sign = gain_sign[:, b * PACK : (b + 1) * PACK].rearrange("p (u e) -> p u e", e=2)
-            nc.vector.tensor_tensor(
-                tile[:].rearrange("p (j u e) -> p j u e", u=2, e=2),
-                src,
-                sign.unsqueeze(1).to_broadcast([P, c1 - c0, 2, 2]),
-                ALU.mult,
-            )
-            h_il[(b, half, c0)] = tile
-
-        def quantize_h(b, half, c0=0, c1=BANK):
-            if c0 == 0:
-                h_c[(b, half)] = keep.tile([P, BANK], U32, name="h_c%d%d" % (b, half), align_bytes=64)
-                h_s[(b, half)] = keep.tile([P, BANK], U8, name="h_s%d%d" % (b, half), align_bytes=64)
-            nc.vector.quantize_mx(
-                out=h_c[(b, half)][:, c0:c1].bitcast(E4M3X4), scales=h_s[(b, half)][:, c0:c1], in_=h_il[(b, half, c0)][:]
-            )
-
-        e_sb = keep.tile([P, PACK, S], F32, name="e_sb")
-        e_ps = {}
-
-        def second_product(t, half, b, c0=0, c1=BANK):
-            if b == 0:
-                e_ps[(t, half)] = psum.tile([P, BANK], F32, name="e%d%d" % (t, half), tag="bank%d" % (t * HALVES + half))
-            nc.tensor.matmul_mx(
-                out=e_ps[(t, half)][:, c0:c1],
-                lhsT=w2_c[:, b, 2 * t * P : 2 * (t + 1) * P].bitcast(E2M1X4),
-                lhsT_scale=w2_s[:, b, t * P : (t + 1) * P],
-                rhs=h_c[(b, half)][:, c0:c1].bitcast(E4M3X4),
-                rhs_scale=h_s[(b, half)][:, c0:c1],
-                start=(b == 0),
-                stop=(b == H_PASSES - 1 and c1 == BANK),
-            )
-
-        def evacuate(t, half):
-            nc.scalar.copy(out=e_sb[:, t, half * BANK : (half + 1) * BANK], in_=e_ps[(t, half)][:])
-
-        for a in range(last):
-            gather_words(a)
-            if a == 0:
-                nc.vector.tensor_copy(v_s[:], tab_s[:].indirect(offs_sb[:]))
+        gather_words(0, 0, S)
+        quantize_w1(0, 0, round_w1(0, 0, nc.scalar.copy))
+        quantize_w1(1, 0, round_w1(1, 0, nc.scalar.copy, tag="shared", bufs=1))
+        v_s = ring.tile([P, S], U8, name="v_s", tag="shared", bufs=1, align_bytes=64)
+        nc.vector.tensor_copy(v_s[:], tab_s[:].indirect(offs_sb[:]))
+        for half in range(HALVES):
+            first_product(v_s, 0, half, 0)
+        for a in range(1, LAST_K):
+            gather_words(a, 0, S)
             for b in range(H_PASSES):
-                quantize_w1(b, a, round_w1(b, a, 0))
-            first_pass(0, a)
+                quantize_w1(b, a, round_w1(b, a, nc.scalar.copy))
+            for half in range(HALVES):
+                first_product(v_s, 0, half, a)
+
+        w2_c = keep.tile([P, H_PASSES, 2 * N], U8, name="w2_c", align_bytes=64)
+        w2_s = keep.tile([P, H_PASSES, N], U8, name="w2_s", align_bytes=64)
         for b in range(H_PASSES):
             nc.vector.tensor_copy(
-                out=w2_c[:, b, :].rearrange("p (t q e) -> p t q e", t=PACK, e=2),
-                in_=w2_raw[:, b, :].rearrange("p (q t e) -> p t q e", t=PACK, e=2),
+                out=w2_c[:, b, :].rearrange("p (t m x) -> p t m x", t=PACK, x=2),
+                in_=w2_raw[:, b, :].rearrange("p (m t x) -> p t m x", t=PACK, x=2),
             )
         nc.vector.tensor_copy(
-            out=w2_s[:].rearrange("p b (t q) -> p b t q", t=PACK),
-            in_=w2s_raw[:].rearrange("p b (q t) -> p b t q", t=PACK),
+            out=w2_s[:].rearrange("p b (t m) -> p b t m", t=PACK),
+            in_=w2s_raw[:].rearrange("p b (m t) -> p b t m", t=PACK),
         )
-        quantize_w1(0, last, round_w1(0, last, 128))
+
+        quantize_w1(0, LAST_K, round_w1(0, LAST_K, nc.vector.tensor_copy))
         for half in range(HALVES):
-            gather_words(last, half * BANK, (half + 1) * BANK)
+            gather_words(LAST_K, half * BANK, (half + 1) * BANK)
+            first_product(v_s, 0, half, LAST_K)
+
+        h_pairs = [ring.tile([P, 2, S, 2], BF16, name="h_pairs%d" % b, tag="h_pairs") for b in range(H_PASSES)]
+        h_c = {}
+        h_s = {}
+        e_ps = {}
+        e_turns = keep.tile([P, PACK, S], F32, name="e_turns")
+
+        def distance(b, half):
             for t in range(PACK):
-                first_product(0, t, half, last)
+                d = target_sb[(b, t, half)]
+                nc.vector.tensor_tensor(d, acc[(b, t, half)][:], d, ALU.subtract)
+                pairs = h_pairs[b][:, t // 2, half * BANK : (half + 1) * BANK, t % 2]
+                nc.scalar.activation(pairs, d, ACT.Abs, scale=gain_sb[:, b, t : t + 1])
+
+        def quantize_h(b, half):
+            woven = ring.tile([P, PACK * BANK], BF16, name="h_woven%d%d" % (b, half), tag="h_woven", bufs=1, align_bytes=64)
+            sign = gain_sign[:, b * PACK : (b + 1) * PACK].rearrange("p (u e) -> p u e", e=2)
+            nc.vector.tensor_tensor(
+                woven[:].rearrange("p (j u e) -> p j u e", u=2, e=2),
+                h_pairs[b][:, :, half * BANK : (half + 1) * BANK, :].rearrange("p u j e -> p j u e"),
+                sign.unsqueeze(1).to_broadcast([P, BANK, 2, 2]),
+                ALU.mult,
+            )
+            h_c[(b, half)] = keep.tile([P, BANK], U32, name="h_c%d%d" % (b, half), align_bytes=64)
+            h_s[(b, half)] = keep.tile([P, BANK], U8, name="h_s%d%d" % (b, half), align_bytes=64)
+            nc.vector.quantize_mx(out=h_c[(b, half)][:].bitcast(E4M3X4), scales=h_s[(b, half)][:], in_=woven[:])
+
+        def second_product(t, half, b):
+            if b == 0:
+                e_ps[(t, half)] = bank("e%d%d" % (t, half), t, half)
+            nc.tensor.matmul_mx(
+                out=e_ps[(t, half)][:],
+                lhsT=w2_c[:, b, 2 * t * P : 2 * (t + 1) * P].bitcast(E2M1X4),
+                lhsT_scale=w2_s[:, b, t * P : (t + 1) * P],
+                rhs=h_c[(b, half)][:].bitcast(E4M3X4),
+                rhs_scale=h_s[(b, half)][:],
+                start=(b == 0),
+                stop=(b == H_PASSES - 1),
+            )
 
         distance(0, 0)
-        for a in range(last):
-            for t in range(PACK):
-                first_product(1, t, 0, a)
-        grouped = round_w1(1, last, 64)
+        for a in range(LAST_K):
+            first_product(v_s, 1, 0, a)
+        w1_final = round_w1(1, LAST_K, nc.vector.tensor_copy)
         distance(0, 1)
-        for a in range(last):
-            for t in range(PACK):
-                first_product(1, t, 1, a)
-
-        quantize_w1(1, last, grouped, 4)
-        first_pass(1, last)
-        interleave_h(0, 0)
-        quantize_h(0, 0)
-        distance(1, 0)
-        interleave_h(0, 1)
-        quantize_h(0, 1)
-        distance(1, 1, 512)
+        for a in range(LAST_K):
+            first_product(v_s, 1, 1, a)
+        quantize_w1(1, LAST_K, w1_final, width=P)
+        for half in range(HALVES):
+            first_product(v_s, 1, half, LAST_K)
+        for half in range(HALVES):
+            quantize_h(0, half)
+            distance(1, half)
         for half in range(HALVES):
             for t in range(PACK):
                 second_product(t, half, 0)
-        interleave_h(1, 0)
-        quantize_h(1, 0)
-        for t in range(PACK):
-            second_product(t, 0, 1)
-            evacuate(t, 0)
-        for c0 in range(0, BANK, 512):
-            interleave_h(1, 1, c0, c0 + 512)
-            quantize_h(1, 1, c0, c0 + 512)
+        for half in range(HALVES):
+            quantize_h(1, half)
             for t in range(PACK):
-                for n0 in range(c0, c0 + 512, 512):
-                    second_product(t, 1, 1, n0, n0 + 512)
-                if c0 + 512 == BANK:
-                    evacuate(t, 1)
+                second_product(t, half, 1)
+                columns = e_turns[:, t, half * BANK : (half + 1) * BANK]
+                nc.scalar.activation(columns, e_ps[(t, half)][:], ACT.Copy, scale=1.0 / TURN)
 
         y_c = keep.tile([P, M], U32, name="y_c", align_bytes=64)
         y_s = keep.tile([P, M], U8, name="y_s", align_bytes=64)
+        y = keep.tile([P, PACK, M], F32, name="y")
+        y_woven = keep.tile([P, PACK * M], BF16, name="y_woven", align_bytes=64)
         out_rows = out_0.rearrange("(p t) m -> p t m", t=PACK)
         out_words = out_1[0].rearrange("p m i -> p (m i)").bitcast(I32)
-        y = keep.tile([P, PACK, M], F32, name="y")
-        y_il = keep.tile([P, PACK * M], BF16, name="y_il", align_bytes=64)
-        pair = {}
-        turns = {}
 
-        def pick(t, m0, m1):
-            if m0 == 0:
-                pair[t] = ring.tile([P, 2, M], F32, name="pair%d" % t, tag="tgt", bufs=4)
-                turns[t] = ring.tile([P, M], I32, name="turns%d" % t, tag="narrow")
-            for side in range(2):
-                nc.vector.tensor_copy(pair[t][:, side, m0:m1], e_sb[:, t, :].indirect(pos_sb[side][:, m0 // 16 : m1 // 16]))
+        def pair_tiles(t):
+            pair = ring.tile([P, 2, M], F32, name="pair%d" % t, tag="rows", bufs=4)
+            whole = ring.tile([P, M], I32, name="whole%d" % t, tag="narrow")
+            return pair[:, 0, :], pair[:, 1, :], whole[:]
 
-        def reduce_angle(t, m0, m1):
-            low, frac, whole = pair[t][:, 0, m0:m1], pair[t][:, 1, m0:m1], turns[t][:, m0:m1]
-            nc.vector.tensor_tensor(low, low, frac, ALU.min)
-            if t < 3:
-                nc.scalar.activation(whole.bitcast(U32), low, ACT.Copy, scale=0.5 / math.pi, bias=ROUNDING)
-                nc.scalar.activation(frac, whole.bitcast(U32), ACT.Copy, scale=1.0, bias=-ROUNDING)
-                nc.vector.scalar_tensor_tensor(frac, low, 0.5 / math.pi, frac, ALU.mult, ALU.subtract)
-            else:
-                nc.vector.tensor_scalar(whole, low, 0.5 / math.pi, None, ALU.mult)
-                nc.vector.scalar_tensor_tensor(frac, low, 0.5 / math.pi, whole, ALU.mult, ALU.subtract)
-            nc.scalar.activation(frac, frac, ACT.Sin, scale=2.0 * math.pi)
+        def pick_smaller(t, low, other, m0, m1):
+            for dst, pos in zip((low, other), pos_sb):
+                offsets = pos[:, m0 // LIST_ROWS : m1 // LIST_ROWS]
+                nc.vector.tensor_copy(dst[:, m0:m1], e_turns[:, t, :].indirect(offsets))
+            nc.vector.tensor_tensor(low[:, m0:m1], low[:, m0:m1], other[:, m0:m1], ALU.min)
 
-        def scale_low(t, m0, m1):
-            nc.scalar.activation(y[:, t, m0:m1], pair[t][:, 0, m0:m1], ACT.Copy, scale=sluice_sb[:, t : t + 1])
+        def turned_sum(name, t, i, sources):
+            total = bank(name, t, i)
+            for m0 in range(0, M, P):
+                for place, source in enumerate(sources):
+                    nc.tensor.matmul(
+                        total[:, m0 : m0 + P],
+                        source[:, m0 : m0 + P],
+                        identity[:],
+                        start=(place == 0),
+                        stop=(place == len(sources) - 1),
+                        is_transpose=True,
+                    )
+            return total
 
-        def add_on_vector(t, m0, m1):
+        def scale_low(t, low, m0, m1):
+            nc.scalar.activation(y[:, t, m0:m1], low[:, m0:m1], ACT.Copy, scale=sluice_turn[:, t : t + 1])
+
+        def add_sine(t, sine, m0, m1):
             nc.vector.scalar_tensor_tensor(
-                y[:, t, m0:m1], pair[t][:, 1, m0:m1], sluice_sb[:, t : t + 1], y[:, t, m0:m1], ALU.mult, ALU.add
+                y[:, t, m0:m1], sine[:, m0:m1], sluice_sb[:, t : t + 1], y[:, t, m0:m1], ALU.mult, ALU.add
             )
             nc.sync.dma_start(out=out_rows[:, t, m0:m1], in_=y[:, t, m0:m1])
 
-        def interleave_y(m0, m1, vector_share):
-            dst = y_il[:, PACK * m0 : PACK * m1].rearrange("p (c i t) -> p c t i", i=4, t=PACK)
-            shared_copy(dst, y[:, :, m0:m1].rearrange("p t (c i) -> p c t i", i=4), vector_share)
-
-        def planes(m0, m1):
-            nc.vector.quantize_mx(
-                out=y_c[:, m0:m1].bitcast(E4M3X4), scales=y_s[:, m0:m1], in_=y_il[:, PACK * m0 : PACK * m1]
-            )
-
-        def store_words(m0, m1):
-            nc.sync.dma_start(out=out_words[:, m0:m1], in_=y_c[:, m0:m1].bitcast(I32))
-
         final = PACK - 1
-        parts = ((0, 256), (256, M))
         for t in range(final):
-            pick(t, 0, M)
-            reduce_angle(t, 0, M)
-            scale_low(t, 0, M)
-            add_on_vector(t, 0, M)
-        for part in parts:
-            pick(final, *part)
-            reduce_angle(final, *part)
-            scale_low(final, *part)
-        for part in parts:
-            add_on_vector(final, *part)
-        interleave_y(*parts[0], 0)
-        interleave_y(*parts[1], (M - 256) // 4)
-        for m0, m1 in parts:
-            for c0 in range(m0, m1, 256):
-                planes(c0, min(m1, c0 + 256))
-            store_words(m0, m1)
+            low, other, whole = pair_tiles(t)
+            pick_smaller(t, low, other, 0, M)
+            nc.scalar.activation(whole.bitcast(U32), low, ACT.Copy, scale=1.0, bias=ROUNDING)
+            nc.scalar.activation(other, whole.bitcast(U32), ACT.Copy, scale=-1.0, bias=ROUNDING)
+            fraction_turned = turned_sum("fraction_turned%d" % t, t, 0, [low, other])
+            sine_turned = ring.tile([P, M], F32, name="sine_turned%d" % t, tag="wide")
+            nc.scalar.activation(sine_turned[:], fraction_turned[:], ACT.Sin, scale=TURN)
+            sine = turned_sum("sine%d" % t, t, 1, [sine_turned[:]])
+            scale_low(t, low, 0, M)
+            add_sine(t, sine[:], 0, M)
 
-        for q in range(4):
+        parts = ((0, M // 2), (M // 2, M))
+        low, other, whole = pair_tiles(final)
+        for m0, m1 in parts:
+            pick_smaller(final, low, other, m0, m1)
+            nc.vector.tensor_copy(whole[:, m0:m1], low[:, m0:m1])
+            nc.vector.tensor_tensor(other[:, m0:m1], low[:, m0:m1], whole[:, m0:m1], ALU.subtract)
+            nc.scalar.activation(other[:, m0:m1], other[:, m0:m1], ACT.Sin, scale=TURN)
+            scale_low(final, low, m0, m1)
+        for m0, m1 in parts:
+            add_sine(final, other, m0, m1)
+
+        for (m0, m1), copy in zip(parts, (nc.scalar.copy, nc.vector.tensor_copy)):
+            copy(
+                out=y_woven[:, PACK * m0 : PACK * m1].rearrange("p (c i t) -> p c t i", i=4, t=PACK),
+                in_=y[:, :, m0:m1].rearrange("p t (c i) -> p c t i", i=4),
+            )
+        for m0, m1 in parts:
+            nc.vector.quantize_mx(
+                out=y_c[:, m0:m1].bitcast(E4M3X4), scales=y_s[:, m0:m1], in_=y_woven[:, PACK * m0 : PACK * m1]
+            )
+            nc.sync.dma_start(out=out_words[:, m0:m1], in_=y_c[:, m0:m1].bitcast(I32))
+        for q in range(QUADRANTS):
             queue = nc.scalar if q % 2 else nc.sync
             queue.dma_start(
                 out=out_2[0, 4 * q : 4 * q + 4, :].bitcast(I32), in_=y_s[32 * q : 32 * q + 4, :].bitcast(I32)

@@ -29,6 +29,7 @@ HALVES = S // BANK
 QUADRANTS = 4
 LIST_ROWS = 16
 TURN = 2.0 * math.pi
+TURNED_SETS = 2
 ROUNDING = 1.5 * 2.0**23
 
 
@@ -303,12 +304,17 @@ def tile_list_salt_pan_pairs_kernel(
             pick_smaller(t, low, other, 0, M)
             nc.scalar.activation(whole.bitcast(U32), low, ACT.Copy, scale=1.0, bias=ROUNDING)
             nc.scalar.activation(other, whole.bitcast(U32), ACT.Copy, scale=-1.0, bias=ROUNDING)
-            fraction_turned = turned_sum("fraction_turned%d" % t, t, 0, [low, other])
-            sine_turned = ring.tile([P, M], F32, name="sine_turned%d" % t, tag="wide")
-            nc.scalar.activation(sine_turned[:], fraction_turned[:], ACT.Sin, scale=TURN)
-            sine = turned_sum("sine%d" % t, t, 1, [sine_turned[:]])
+            if t < TURNED_SETS:
+                fraction_turned = turned_sum("fraction_turned%d" % t, t, 0, [other, low])
+                sine_turned = ring.tile([P, M], F32, name="sine_turned%d" % t, tag="wide")
+                nc.scalar.activation(sine_turned[:], fraction_turned[:], ACT.Sin, scale=TURN)
+                sine = turned_sum("sine%d" % t, t, 1, [sine_turned[:]])[:]
+            else:
+                nc.vector.tensor_tensor(other, low, other, ALU.add)
+                nc.scalar.activation(other, other, ACT.Sin, scale=TURN)
+                sine = other
             scale_low(t, low, 0, M)
-            add_sine(t, sine[:], 0, M)
+            add_sine(t, sine, 0, M)
 
         parts = ((0, M // 2), (M // 2, M))
         low, other, whole = pair_tiles(final)
@@ -321,7 +327,13 @@ def tile_list_salt_pan_pairs_kernel(
         for m0, m1 in parts:
             add_sine(final, other, m0, m1)
 
-        for (m0, m1), copy in zip(parts, (nc.scalar.copy, nc.vector.tensor_copy)):
+        quarter = M // 4
+        shares = (
+            (nc.scalar.copy, quarter, 2 * quarter),
+            (nc.vector.tensor_copy, 0, quarter),
+            (nc.vector.tensor_copy, 2 * quarter, M),
+        )
+        for copy, m0, m1 in shares:
             copy(
                 out=y_woven[:, PACK * m0 : PACK * m1].rearrange("p (c i t) -> p c t i", i=4, t=PACK),
                 in_=y[:, :, m0:m1].rearrange("p t (c i) -> p c t i", i=4),

import math
from contextlib import ExitStack

import concourse.mybir as mybir
from concourse.masks import make_identity

K, H, N, T, S, M = 1536, 1024, 512, 4096, 1024, 512
FLOPS = 2 * K * H * S + 2 * H * N * S

F32 = mybir.dt.float32
BF16 = mybir.dt.bfloat16
I32 = mybir.dt.int32
U32 = mybir.dt.uint32
U16 = mybir.dt.uint16
U8 = mybir.dt.uint8
E4M3X4 = mybir.dt.float8_e4m3fn_x4
E2M1X4 = mybir.dt.float4_e2m1fn_x4
ALU = mybir.AluOpType
ACT = mybir.ActivationFunctionType

P = 128
PACK = 4
PASS = P * PACK
K_PASSES = K // PASS
H_PASSES = H // PASS
LAST_K = K_PASSES - 1
BANK = 512
HALVES = S // BANK
QUADRANTS = 4
LIST_ROWS = 16
TURN = 2.0 * math.pi
TURNED_SETS = 2
ROUNDING = 1.5 * 2.0**23


def tile_list_salt_pan_pairs_kernel(
    tc, tab_words, tab_scales, offs, w1, target, gain, w2_words, w2_scales, pos1, pos2, sluice, out_0, out_1, out_2
):
    nc = tc.nc
    with ExitStack() as ctx:
        keep = ctx.enter_context(tc.tile_pool(name="keep", bufs=1))
        ring = ctx.enter_context(tc.tile_pool(name="ring", bufs=2))
        psum = ctx.enter_context(tc.psum_pool(name="psum", bufs=1))

        def bank(name, t, i):
            return psum.tile([P, BANK], F32, name=name, tag="bank%d" % (HALVES * t + i))

        offs_sb = keep.tile([P, S // LIST_ROWS], U16, name="offs_sb")
        pos_sb = [keep.tile([P, M // LIST_ROWS], U16, name="pos%d_sb" % side) for side in (1, 2)]
        tab_w = [keep.tile([P, T], I32, name="tab_w%d" % a) for a in range(K_PASSES)]
        tab_s = keep.tile([P, T], U8, name="tab_s")
        w2_raw = keep.tile([P, H_PASSES, 2 * N], U8, name="w2_raw")
        w2s_raw = keep.tile([P, H_PASSES, N], U8, name="w2s_raw")
        gain_sb = keep.tile([P, H_PASSES, PACK], F32, name="gain_sb")
        sluice_sb = keep.tile([P, PACK], F32, name="sluice_sb")

        nc.vector.memset(tab_s[:].bitcast(I32), 0)
        nc.vector.memset(w2s_raw[:].bitcast(I32), 0)
        nc.sync.dma_start(offs_sb[:], offs)
        nc.scalar.dma_start(out=gain_sb[:], in_=gain.rearrange("(b p t) -> p b t", b=H_PASSES, t=PACK))
        nc.scalar.dma_start(out=sluice_sb[:], in_=sluice.rearrange("(p t) -> p t", t=PACK))

        w1_raw = {}
        target_sb = {}

        def load_table(a):
            nc.sync.dma_start(out=tab_w[a][:], in_=tab_words[a].rearrange("p t i -> p (t i)").bitcast(I32))

        def load_w1_rows(a):
            raw = ring.tile([P, PACK, H], F32, name="w1_rows%d" % a, tag="wide")
            nc.sync.dma_start(out=raw[:], in_=w1[a * PASS : (a + 1) * PASS, :].rearrange("(p i) c -> p i c", i=PACK))
            for b in range(H_PASSES):
                w1_raw[(b, a)] = raw[:, :, b * PASS : (b + 1) * PASS]

        def load_w1_block(b, a):
            raw = ring.tile([P, PACK, PASS], F32, name="w1_raw%d%d" % (b, a), tag="narrow")
            rows = w1[a * PASS : (a + 1) * PASS, b * PASS : (b + 1) * PASS]
            nc.sync.dma_start(out=raw[:], in_=rows.rearrange("(p i) c -> p i c", i=PACK))
            w1_raw[(b, a)] = raw[:]

        def load_target(b, u):
            tile = ring.tile([P, 2, S], F32, name="target%d%d" % (b, u), tag="rows", bufs=4)
            rows = target[b * PASS : (b + 1) * PASS, :].rearrange("(p t) j -> p t j", t=PACK)
            nc.sync.dma_start(out=tile[:], in_=rows[:, 2 * u : 2 * u + 2, :])
            for e in range(2):
                for half in range(HALVES):
                    target_sb[(b, 2 * u + e, half)] = tile[:, e, half * BANK : (half + 1) * BANK]

        load_table(0)
        for q in range(QUADRANTS):
            nc.gpsimd.dma_start(
                out=tab_s[32 * q : 32 * q + 4 * K_PASSES, :].bitcast(I32),
                in_=tab_scales[:, 4 * q : 4 * q + 4, :].bitcast(I32),
            )
        nc.sync.dma_start(out=w2_raw[:].bitcast(I32), in_=w2_words.rearrange("b p c -> p b c").bitcast(I32))
        for q in range(QUADRANTS):
            nc.sync.dma_start(
                out=w2s_raw[32 * q : 32 * q + 4, :, :].bitcast(I32),
                in_=w2_scales[:, 4 * q : 4 * q + 4, :].rearrange("b r c -> r b c").bitcast(I32),
            )
        for a in range(LAST_K):
            load_w1_rows(a)
            if a + 1 < LAST_K:
                load_table(a + 1)
        load_w1_block(0, LAST_K)
        load_table(LAST_K)
        load_target(0, 0)
        load_target(0, 1)
        load_w1_block(1, LAST_K)
        load_target(1, 0)
        load_target(1, 1)
        nc.sync.dma_start(pos_sb[0][:], pos1)
        nc.sync.dma_start(pos_sb[1][:], pos2)

        gain_half = keep.tile([P, H_PASSES * PACK], F32, name="gain_half")
        gain_sign = keep.tile([P, H_PASSES * PACK], BF16, name="gain_sign")
        nc.vector.tensor_scalar(gain_half[:], gain_sb[:].rearrange("p b t -> p (b t)"), 0.0, -0.5, ALU.is_ge, ALU.add)
        nc.scalar.activation(gain_sign[:], gain_half[:], ACT.Sin, scale=math.pi)
        identity = keep.tile([P, P], F32, name="identity")
        make_identity(nc, identity[:])
        sluice_turn = keep.tile([P, PACK], F32, name="sluice_turn")
        nc.vector.tensor_scalar(sluice_turn[:], sluice_sb[:], TURN, None, ALU.mult)

        v_w = [keep.tile([P, S], U32, name="v_w%d" % a, align_bytes=64) for a in range(K_PASSES)]
        w1_c = {}
        w1_s = {}
        acc = {}

        def gather_words(a, j0, j1):
            offsets = offs_sb[:, j0 // LIST_ROWS : j1 // LIST_ROWS]
            nc.vector.tensor_copy(v_w[a][:, j0:j1], tab_w[a][:].bitcast(U32).indirect(offsets))

        def round_w1(b, a, copy, tag="w1_bf", bufs=2):
            grouped = ring.tile([P, PACK * PASS], BF16, name="w1_bf%d%d" % (b, a), tag=tag, bufs=bufs, align_bytes=64)
            copy(
                out=grouped[:].rearrange("p (t m i) -> p m i t", t=PACK, i=PACK),
                in_=w1_raw[(b, a)].rearrange("p i (m t) -> p m i t", t=PACK),
            )
            return grouped

        def quantize_w1(b, a, grouped, width=PASS):
            w1_c[(b, a)] = keep.tile([P, PASS], U32, name="w1_c%d%d" % (b, a), align_bytes=64)
            w1_s[(b, a)] = keep.tile([P, PASS], U8, name="w1_s%d%d" % (b, a), align_bytes=64)
            for c0 in range(0, PASS, width):
                cols = slice(c0, c0 + width)
                nc.vector.quantize_mx(
                    out=w1_c[(b, a)][:, cols].bitcast(E4M3X4),
                    scales=w1_s[(b, a)][:, cols],
                    in_=grouped[:, PACK * c0 : PACK * (c0 + width)],
                )

        def first_product(v_s, b, half, a):
            cols = slice(half * BANK, (half + 1) * BANK)
            for t in range(PACK):
                if a == 0:
                    acc[(b, t, half)] = bank("acc%d%d%d" % (b, t, half), t, half)
                nc.tensor.matmul_mx(
                    out=acc[(b, t, half)][:],
                    lhsT=w1_c[(b, a)][:, t * P : (t + 1) * P].bitcast(E4M3X4),
                    lhsT_scale=w1_s[(b, a)][:, t * P : (t + 1) * P],
                    rhs=v_w[a][:, cols].bitcast(E4M3X4),
                    rhs_scale=v_s[4 * a : P, cols],
                    start=(a == 0),
                    stop=(a == LAST_K),
                )

        gather_words(0, 0, S)
        quantize_w1(0, 0, round_w1(0, 0, nc.scalar.copy))
        quantize_w1(1, 0, round_w1(1, 0, nc.scalar.copy, tag="shared", bufs=1))
        v_s = ring.tile([P, S], U8, name="v_s", tag="shared", bufs=1, align_bytes=64)
        nc.vector.tensor_copy(v_s[:], tab_s[:].indirect(offs_sb[:]))
        for half in range(HALVES):
            first_product(v_s, 0, half, 0)
        for a in range(1, LAST_K):
            gather_words(a, 0, S)
            for b in range(H_PASSES):
                quantize_w1(b, a, round_w1(b, a, nc.scalar.copy))
            for half in range(HALVES):
                first_product(v_s, 0, half, a)

        w2_c = keep.tile([P, H_PASSES, 2 * N], U8, name="w2_c", align_bytes=64)
        w2_s = keep.tile([P, H_PASSES, N], U8, name="w2_s", align_bytes=64)
        for b in range(H_PASSES):
            nc.vector.tensor_copy(
                out=w2_c[:, b, :].rearrange("p (t m x) -> p t m x", t=PACK, x=2),
                in_=w2_raw[:, b, :].rearrange("p (m t x) -> p t m x", t=PACK, x=2),
            )
        nc.vector.tensor_copy(
            out=w2_s[:].rearrange("p b (t m) -> p b t m", t=PACK),
            in_=w2s_raw[:].rearrange("p b (m t) -> p b t m", t=PACK),
        )

        quantize_w1(0, LAST_K, round_w1(0, LAST_K, nc.vector.tensor_copy))
        for half in range(HALVES):
            gather_words(LAST_K, half * BANK, (half + 1) * BANK)
            first_product(v_s, 0, half, LAST_K)

        h_pairs = [ring.tile([P, 2, S, 2], BF16, name="h_pairs%d" % b, tag="h_pairs") for b in range(H_PASSES)]
        h_c = {}
        h_s = {}
        e_ps = {}
        e_turns = keep.tile([P, PACK, S], F32, name="e_turns")

        def distance(b, half):
            for t in range(PACK):
                d = target_sb[(b, t, half)]
                nc.vector.tensor_tensor(d, acc[(b, t, half)][:], d, ALU.subtract)
                pairs = h_pairs[b][:, t // 2, half * BANK : (half + 1) * BANK, t % 2]
                nc.scalar.activation(pairs, d, ACT.Abs, scale=gain_sb[:, b, t : t + 1])

        def quantize_h(b, half):
            woven = ring.tile([P, PACK * BANK], BF16, name="h_woven%d%d" % (b, half), tag="h_woven", bufs=1, align_bytes=64)
            sign = gain_sign[:, b * PACK : (b + 1) * PACK].rearrange("p (u e) -> p u e", e=2)
            nc.vector.tensor_tensor(
                woven[:].rearrange("p (j u e) -> p j u e", u=2, e=2),
                h_pairs[b][:, :, half * BANK : (half + 1) * BANK, :].rearrange("p u j e -> p j u e"),
                sign.unsqueeze(1).to_broadcast([P, BANK, 2, 2]),
                ALU.mult,
            )
            h_c[(b, half)] = keep.tile([P, BANK], U32, name="h_c%d%d" % (b, half), align_bytes=64)
            h_s[(b, half)] = keep.tile([P, BANK], U8, name="h_s%d%d" % (b, half), align_bytes=64)
            nc.vector.quantize_mx(out=h_c[(b, half)][:].bitcast(E4M3X4), scales=h_s[(b, half)][:], in_=woven[:])

        def second_product(t, half, b):
            if b == 0:
                e_ps[(t, half)] = bank("e%d%d" % (t, half), t, half)
            nc.tensor.matmul_mx(
                out=e_ps[(t, half)][:],
                lhsT=w2_c[:, b, 2 * t * P : 2 * (t + 1) * P].bitcast(E2M1X4),
                lhsT_scale=w2_s[:, b, t * P : (t + 1) * P],
                rhs=h_c[(b, half)][:].bitcast(E4M3X4),
                rhs_scale=h_s[(b, half)][:],
                start=(b == 0),
                stop=(b == H_PASSES - 1),
            )

        distance(0, 0)
        for a in range(LAST_K):
            first_product(v_s, 1, 0, a)
        w1_final = round_w1(1, LAST_K, nc.vector.tensor_copy)
        distance(0, 1)
        for a in range(LAST_K):
            first_product(v_s, 1, 1, a)
        quantize_w1(1, LAST_K, w1_final, width=P)
        for half in range(HALVES):
            first_product(v_s, 1, half, LAST_K)
        for half in range(HALVES):
            quantize_h(0, half)
            distance(1, half)
        for half in range(HALVES):
            for t in range(PACK):
                second_product(t, half, 0)
        for half in range(HALVES):
            quantize_h(1, half)
            for t in range(PACK):
                second_product(t, half, 1)
                columns = e_turns[:, t, half * BANK : (half + 1) * BANK]
                nc.scalar.activation(columns, e_ps[(t, half)][:], ACT.Copy, scale=1.0 / TURN)

        y_c = keep.tile([P, M], U32, name="y_c", align_bytes=64)
        y_s = keep.tile([P, M], U8, name="y_s", align_bytes=64)
        y = keep.tile([P, PACK, M], F32, name="y")
        y_woven = keep.tile([P, PACK * M], BF16, name="y_woven", align_bytes=64)
        out_rows = out_0.rearrange("(p t) m -> p t m", t=PACK)
        out_words = out_1[0].rearrange("p m i -> p (m i)").bitcast(I32)

        def pair_tiles(t):
            pair = ring.tile([P, 2, M], F32, name="pair%d" % t, tag="rows", bufs=4)
            whole = ring.tile([P, M], I32, name="whole%d" % t, tag="narrow")
            return pair[:, 0, :], pair[:, 1, :], whole[:]

        def pick_smaller(t, low, other, m0, m1):
            for dst, pos in zip((low, other), pos_sb):
                offsets = pos[:, m0 // LIST_ROWS : m1 // LIST_ROWS]
                nc.vector.tensor_copy(dst[:, m0:m1], e_turns[:, t, :].indirect(offsets))
            nc.vector.tensor_tensor(low[:, m0:m1], low[:, m0:m1], other[:, m0:m1], ALU.min)

        def turned_sum(name, t, i, sources):
            total = bank(name, t, i)
            for m0 in range(0, M, P):
                for place, source in enumerate(sources):
                    nc.tensor.matmul(
                        total[:, m0 : m0 + P],
                        source[:, m0 : m0 + P],
                        identity[:],
                        start=(place == 0),
                        stop=(place == len(sources) - 1),
                        is_transpose=True,
                    )
            return total

        def scale_low(t, low, m0, m1):
            nc.scalar.activation(y[:, t, m0:m1], low[:, m0:m1], ACT.Copy, scale=sluice_turn[:, t : t + 1])

        def add_sine(t, sine, m0, m1):
            nc.vector.scalar_tensor_tensor(
                y[:, t, m0:m1], sine[:, m0:m1], sluice_sb[:, t : t + 1], y[:, t, m0:m1], ALU.mult, ALU.add
            )
            nc.sync.dma_start(out=out_rows[:, t, m0:m1], in_=y[:, t, m0:m1])

        final = PACK - 1
        for t in range(final):
            low, other, whole = pair_tiles(t)
            pick_smaller(t, low, other, 0, M)
            nc.scalar.activation(whole.bitcast(U32), low, ACT.Copy, scale=1.0, bias=ROUNDING)
            nc.scalar.activation(other, whole.bitcast(U32), ACT.Copy, scale=-1.0, bias=ROUNDING)
            if t < TURNED_SETS:
                fraction_turned = turned_sum("fraction_turned%d" % t, t, 0, [other, low])
                sine_turned = ring.tile([P, M], F32, name="sine_turned%d" % t, tag="wide")
                nc.scalar.activation(sine_turned[:], fraction_turned[:], ACT.Sin, scale=TURN)
                sine = turned_sum("sine%d" % t, t, 1, [sine_turned[:]])[:]
            else:
                nc.vector.tensor_tensor(other, low, other, ALU.add)
                nc.scalar.activation(other, other, ACT.Sin, scale=TURN)
                sine = other
            scale_low(t, low, 0, M)
            add_sine(t, sine, 0, M)

        parts = ((0, M // 2), (M // 2, M))
        low, other, whole = pair_tiles(final)
        for m0, m1 in parts:
            pick_smaller(final, low, other, m0, m1)
            nc.vector.tensor_copy(whole[:, m0:m1], low[:, m0:m1])
            nc.vector.tensor_tensor(other[:, m0:m1], low[:, m0:m1], whole[:, m0:m1], ALU.subtract)
            nc.scalar.activation(other[:, m0:m1], other[:, m0:m1], ACT.Sin, scale=TURN)
            scale_low(final, low, m0, m1)
        for m0, m1 in parts:
            add_sine(final, other, m0, m1)

        quarter = M // 4
        shares = (
            (nc.scalar.copy, quarter, 2 * quarter),
            (nc.vector.tensor_copy, 0, quarter),
            (nc.vector.tensor_copy, 2 * quarter, M),
        )
        for copy, m0, m1 in shares:
            copy(
                out=y_woven[:, PACK * m0 : PACK * m1].rearrange("p (c i t) -> p c t i", i=4, t=PACK),
                in_=y[:, :, m0:m1].rearrange("p t (c i) -> p c t i", i=4),
            )
        for m0, m1 in parts:
            nc.vector.quantize_mx(
                out=y_c[:, m0:m1].bitcast(E4M3X4), scales=y_s[:, m0:m1], in_=y_woven[:, PACK * m0 : PACK * m1]
            )
            nc.sync.dma_start(out=out_words[:, m0:m1], in_=y_c[:, m0:m1].bitcast(I32))
        for q in range(QUADRANTS):
            queue = nc.scalar if q % 2 else nc.sync
            queue.dma_start(
                out=out_2[0, 4 * q : 4 * q + 4, :].bitcast(I32), in_=y_s[32 * q : 32 * q + 4, :].bitcast(I32)
            )
